import numpy as np, ml_dtypes
CORES = [9,25,41,57]
N = 4
BF = ml_dtypes.bfloat16
def gentries(a):
    return np.ascontiguousarray(a.reshape(8, 16, -1).transpose(0, 2, 1)).reshape(8, -1)
def gtable(e):
    e = np.asarray(e); return np.ascontiguousarray(e.reshape(8, -1, 16).transpose(0, 2, 1)).reshape(128, -1).astype(np.int32)
V, G, CAP, RO = 1536, 512, 256, 4
W = V + (N - 1) * G + 17
H = 16 - RO
def parts(rng):
    h = V // 2; S = (N, 8, 16, V)
    o = np.argsort(rng.random(S), axis=-1); a, b = o[..., :h], o[..., h:]
    pool = np.concatenate([b, np.broadcast_to(np.arange(V, W), (N, 8, 16, W - V))], axis=-1)
    pool = np.take_along_axis(pool, np.argsort(rng.random(pool.shape), axis=-1), -1)[..., :V - h]
    nb = np.zeros(S, np.int64)
    np.put_along_axis(nb, o, np.concatenate([a.reshape(N, 8, 16, h // 2, 2)[..., ::-1].reshape(N, 8, 16, h), pool], axis=-1), -1)
    share = rng.permutation(np.array([0.003, 0.003, 0.01, 0.02, 0.05, 0.1, 0.3, 0.6])).reshape(1, 8, 1, 1) * np.exp2(rng.integers(-1, 2, (N, 8, 1, 1)))
    m = (rng.random((N, 8, 1, V)) < share) & (rng.random(S) < 0.5)
    d0 = np.where(m, rng.integers(0, 201, S), 255); nd = rng.integers(1, 64, S); e = rng.random(S)
    lab = np.where(e < 0.3, W - 1, np.where(e < 0.5, rng.integers(W - 17, W - 1, S), rng.integers(0, W - 17, S)))
    hi = rng.permuted(np.tile(np.array([8, 16, 32, 64, 96, 128, 192, 256]), (N, 1)), axis=1).reshape(N, 8, 1, 1)
    ld = (rng.random(S) * hi).astype(np.int64)
    rt = rng.integers(20, 181, (8, 16, 16)); rt[:, np.arange(16), np.arange(16)] = 0; rt = np.tile(rt, (N, 1, 1, 1))
    p = rng.permuted(np.tile(np.array([0.03, 0.05, 0.1, 0.15, 0.2, 0.3, 0.5, 1.0]), (N, 1)), axis=1).reshape(N, 8, 1)
    fl = (rng.random((N, 8, V)) < p).astype(np.int64)
    snd = np.ascontiguousarray(np.argsort(rng.random((N, 8, N - 1, V)), axis=-1)[..., :G])
    return nb, nd, lab, ld, d0, rt, fl, snd
def flat(a, t):
    return np.ascontiguousarray(a.reshape(N, 128, -1)).astype(np.float32).astype(t)
def pack(nb, nd, lab, ld, d0, rt, fl, snd):
    lab = np.array(lab); ld = np.array(ld); lab[:, :, H:] = W - 1; ld[:, :, H:] = 255
    return {"nb": flat(nb, np.int32), "nd": flat(nd, BF), "lab": flat(lab, np.int32), "ld": flat(ld, BF), "d0": flat(d0, BF), "rt": flat(rt, BF),
            "fl": fl.astype(np.int32), "snd": np.stack([gtable(a.reshape(8, -1)) for a in snd])}
def put(row, j, p):
    old = int(row[j]); row[row == p] = old; row[j] = p
def load(rng, nq, nl, lq, dq, fq, sq):
    s = np.nonzero(fq)[0][:CAP]; t = rng.permutation(np.setdiff1d(np.arange(V), s)); T = (N - 1) * G
    sq[:] = rng.permutation(np.concatenate([rng.permutation(s), t])[:G])
    nq[0, s] = t[:CAP]; nq[0, t] = rng.permutation(np.concatenate([t[CAP:], s])); gp = V + rng.permutation(T)
    for i in range(1, 16):
        p = gp[(np.arange(CAP) + (i - 1) * CAP) % T]
        nq[i, s] = p; nq[i, t] = rng.permutation(np.setdiff1d(np.arange(W), p))[:V - CAP]
    nl[:, s] = rng.integers(1, 50, (16, CAP)); lq[:] = W - 1
    dq[:] = 255; dq[:, t[:CAP]] = rng.integers(0, 101, (16, CAP))
def setup_inputs(rng):
    return pack(*parts(rng))
def setup_inputs_room(rng):
    nb, nd, lab, ld, d0, rt, fl, snd = parts(rng); fl[:] = 0
    for q in range(N):
        full = q >= max(1, N // 4)
        for g in range(8):
            n = int(rng.choice(np.array([CAP, CAP + 1, V] if full else [0, 1, CAP - 1, CAP, CAP + 1, V])))
            if q == 0: n = (CAP, CAP + 1, CAP - 1, V, 0, 1, CAP, CAP + 1)[g]
            fl[q, g, rng.permutation(V)[:n]] = 1
            if full: load(rng, nb[q, g], nd[q, g], lab[q, g], d0[q, g], fl[q, g], snd[q, g])
    c = snd[0, 0, 0]; isin = np.zeros(V, np.int64); isin[c] = 1
    o = np.concatenate([rng.permutation(c), rng.permutation(np.nonzero(isin == 0)[0])])
    s, t = o[:CAP], rng.permutation(o[CAP:])
    fl[0, 0] = 0; fl[0, 0, s] = 1
    nb[0, 0, 0, s] = t[:CAP]; nb[0, 0, 0, t] = rng.permutation(np.concatenate([t[CAP:], s]))
    nd[0, 0][:, s] = rng.integers(1, 50, (16, CAP)); lab[0, 0][:, s] = W - 1
    d0[0, 0][:, s] = 255; d0[0, 0][:, t[:CAP]] = rng.integers(0, 101, (16, CAP))
    return pack(nb, nd, lab, ld, d0, rt, fl, snd)
def setup_inputs_ties(rng):
    nb, nd, lab, ld, d0, rt, fl, snd = parts(rng); S = (N, 8, 16, V)
    base = np.array([0, 0, 1, 4, 250, 251, 252, 252]).reshape(1, 8, 1, 1); share = np.array([0.3, 0.1, 0.02, 0.3, 0.02, 0.02, 0.01, 0.005]).reshape(1, 8, 1, 1)
    m = (rng.random((N, 8, 1, V)) < share) & (rng.random(S) < 0.6)
    d0 = np.where(m, base + rng.integers(0, 4, S), 255); nd = rng.integers(0, 3, S); ld = rng.integers(0, 4, S)
    rt = np.minimum(base + rng.integers(0, 5, (N, 8, 16, 16)), 255)
    return pack(nb, nd, lab, ld, d0, rt, fl, snd)
def setup_inputs_alike(rng):
    nb, nd, lab, ld, d0, rt, fl, snd = parts(rng)
    q = int(rng.integers(0, N)); o = rng.permutation(CAP)[:12]; u, x = o[:4], o[4:8]
    for a in range(N):
        d = (a - q) % N; v = o[8:]; p = u
        if d > 0:
            v = rng.permutation(CAP)[:4]; sp = rng.permutation(G)[:4]; p = V + (d - 1) * G + sp
            for j in range(4): put(snd[q, 0, d - 1], sp[j], u[j])
        for j in range(4): put(nb[a, 0, 0], v[j], p[j])
        nd[a, 0][:, v] = rng.integers(1, 50, (16, 4)); lab[a, 0][:, v] = W - 1; d0[a, 0][:, v] = 255; fl[a, 0, v] = 1
    for j in range(4): put(nb[q, 0, 0], u[j], x[j])
    nd[q, 0][:, u] = rng.integers(1, 30, (16, 4)); lab[q, 0][:, u] = W - 1; fl[q, 0, u] = 0
    d0[q, 0][:, u] = rng.integers(60, 101, (16, 4)); d0[q, 0][:, x] = 0
    nb[:, 0] = np.array(nb[:, 0, :1]); nb[:, 1, 0] = np.arange(V); nb[:, 2] = W - 1 - np.arange(V); nb[:, 3] = np.arange(V, 2 * V)
    lab[:, 4] = rng.choice(np.array([0, V - 1, V, W - 18, W - 17, W - 2, W - 1]), (N, 16, V)); lab[:, 5] = np.array(lab[:, 5, :1])
    snd[:, 1::2] = np.array(snd[:, 1::2, :1])
    return pack(nb, nd, lab, ld, d0, rt, fl, snd)
def setup_inputs_quiet(rng):
    nb, nd, lab, ld, d0, rt, fl, snd = parts(rng)
    q = int(rng.integers(0, N)); g = rng.permutation(8); w = fl[q] * 1; fl[:] = 0; fl[q] = w
    fl[q, g[0]] = 0; fl[q, g[1]] = 0; fl[q, g[1], 0] = 1; fl[q, g[1], V - 1] = 1
    h = int(g[2]); fl[q, h] = 1
    for i in range(16):
        p = rng.permutation(CAP) if i == 0 else CAP + rng.permutation(V - CAP)[:CAP]
        nb[q, h, i, :CAP] = p; nb[q, h, i, CAP:] = rng.permutation(np.setdiff1d(np.arange(W), p))[:V - CAP]
    nd[q, h][:, :CAP] = 255; nd[q, h, 1, :CAP] = rng.integers(1, 50, CAP); lab[q, h][:, :CAP + 8] = W - 1
    d0[q, h][:, :CAP] = 255; d0[q, h][:, CAP:] = rng.integers(50, 101, (16, V - CAP)); d0[q, h][:, V - 8:] = 0
    for j in range(8): put(nb[q, h, 0], CAP + j, V - 8 + j)
    nd[q, h, 0, CAP:CAP + 8] = rng.integers(1, 30, 8)
    return pack(nb, nd, lab, ld, d0, rt, fl, snd)
def setup_inputs_spread(rng):
    nb, nd, lab, ld, d0, rt, fl, snd = parts(rng); S = (N, 8, 16, V)
    d0 = np.where(rng.random((N, 8, 1, V)) < 0.2, 255, np.minimum(np.exp2(8 * rng.random((N, 8, 1, V))) * (0.5 + rng.random(S)), 255).astype(np.int64))
    nd = np.minimum(np.exp2(8.1 * rng.random(S)).astype(np.int64) - (rng.random(S) < 0.5), 255)
    ld = np.minimum(np.exp2(8.1 * rng.random(S)).astype(np.int64), 255) * (rng.random(S) < 0.97)
    lab = rng.integers(0, W, S); rt = rng.integers(0, 256, (N, 8, 16, 16))
    fl = (rng.random((N, 8, V)) < rng.random((N, 8, 1)) * rng.random((N, 8, V))).astype(np.int64)
    return pack(nb, nd, lab, ld, d0, rt, fl, snd)
def check_inputs(d):
    bad = []
    for k, lo, hi in (("nb", 0, W - 1), ("lab", 0, W - 1), ("fl", 0, 1), ("snd", 0, V - 1)):
        if np.min(d[k]) < lo or np.max(d[k]) > hi: bad.append("range of " + k)
    for k in ("nd", "ld", "d0", "rt"):
        a = np.asarray(d[k]).astype(np.float32)
        if not np.all((a >= 0) & (a <= 255) & (a == np.floor(a))): bad.append("whole numbers from 0 to 255 in " + k)
    if np.any(np.diff(np.sort(np.asarray(d["nb"]), axis=-1), axis=-1) == 0): bad.append("nb: the numbers of one row differ")
    s = np.stack([gentries(a) for a in np.asarray(d["snd"])]).reshape(N, 8, N - 1, G)
    if np.any(np.diff(np.sort(s, axis=-1), axis=-1) == 0): bad.append("snd: the numbers of one block differ")
    if np.any(np.asarray(d["lab"]).reshape(N, 8, 16, V)[:, :, H:] != W - 1): bad.append("lab: the later entries are the none place")
    if np.any(np.asarray(d["ld"]).astype(np.float32).reshape(N, 8, 16, V)[:, :, H:] != 255): bad.append("ld: the later entries are 255")
    return bad
def ints(a):
    return np.asarray(a).astype(np.float32).astype(np.int64)
def reference(nb, nd, lab, ld, d0, rt, fl, snd):
    S = (N, 8, 16, V); nbl = ints(nb).reshape(S); ndl = ints(nd).reshape(S)
    L = np.array(ints(lab).reshape(S)); M = np.array(ints(ld).reshape(S)); D = np.array(ints(d0).reshape(S))
    R = ints(rt).reshape(N, 8, 16, 16); flag = ints(fl).reshape(N, 8, V) > 0
    sl = np.stack([gentries(a) for a in snd]).astype(np.int64).reshape(N, 8, N - 1, G)
    none = np.full((8, 16, 1), 255, np.int64)
    for t in range(RO):
        F = flag & (np.add.accumulate(flag.astype(np.int64), axis=2) <= CAP)
        flag = flag & ~F
        new = np.array(D); push = np.zeros((N, 8, W), bool)
        for a in range(N):
            guests = [np.take_along_axis(D[(a - d) % N], sl[(a - d) % N, :, d - 1][:, None, :], 2) for d in range(1, N)]
            win = np.concatenate([D[a]] + guests + [R[a], none], axis=2)
            for g in range(8):
                v = np.nonzero(F[a, g])[0]; w = win[g]; old = D[a, g][:, v]
                cand = np.minimum(np.min(w[:, nbl[a, g][:, v]] + ndl[a, g][:, v], axis=1), 255)
                q = np.minimum(np.min(w[:, L[a, g][:, v]] + M[a, g][:, v], axis=1), 255)
                up = (cand < q) & (cand < old); ch = np.any(up, axis=0)
                key = np.where(up, cand, 1000); best = np.argmin(key, axis=0); least = np.min(key, axis=0)
                new[a, g][:, v] = np.where(up, cand, old)
                L[a, g, H + t, v[ch]] = W - 17 + best[ch]; M[a, g, H + t, v[ch]] = least[ch]
                push[a, g, nbl[a, g][:, v[ch]]] = True
        D = new
        for a in range(N):
            flag[a] |= push[a, :, :V]
            for d in range(1, N):
                back = np.zeros((8, V), bool)
                np.put_along_axis(back, sl[(a - d) % N, :, d - 1], push[a, :, V + (d - 1) * G:V + d * G], 1)
                flag[(a - d) % N] |= back
    return {"yd": D.reshape(N, 128, V).astype(np.float32).astype(BF), "yl": L.reshape(N, 128, V).astype(np.float32)}

@@ -1,0 +1,486 @@
+from concourse.bass import DstId, RemoteDMATransfer
+from concourse.mybir import AluOpType, ActivationFunctionType
+
+A = AluOpType
+F = ActivationFunctionType
+N, V, GS, CAP, RO = 4, 1536, 512, 256, 4
+PAD = 288
+NP = V + 3 * GS + 17
+WW = PAD + 3104
+TW = PAD + V
+CW = 3920
+GW = 3376
+NMAT = 22
+
+SCRATCH = {"ps": ("psum", [128, 4096], "float32")}
+for names, width, kind in (
+        ("nbw labi", TW, "int32"), ("labf", TW, "float32"), ("ndw ldw", TW, "bfloat16"),
+        ("fli sni sb sc sd", 96, "int32"), ("snu off", 96, "uint16"), ("su", 192, "uint16"), ("lst", 128, "uint16"),
+        ("sa dumc dum raw fb yy xx beyond rem oc ev es", 96, "float32"), ("fg pl", 96, "bfloat16"),
+        ("x2 xv xs", 192, "float32"),
+        ("cv cs", CW, "float32"), ("vals", V, "float32"), ("gv gs", GW, "float32"), ("ov ow", 3072, "float32"),
+        ("gt sn", 8192, "bfloat16"), ("sbf", V, "bfloat16"), ("mat", NMAT * 128, "bfloat16"),
+        ("pidx pmi gmi", 1, "int32"), ("col", 8, "float32"), ("ci eq wt q1 df", 16, "float32"), ("li", 16, "int32"),
+        ("gl", 16, "uint16"), ("va vb ta tb tc", 128, "float32"), ("blk lt", 128, "bfloat16"),
+        ("r1 r2", 272, "bfloat16"), ("st", 768, "float32"), ("mx zz nb32", 272, "float32"), ("tt", 512, "float32"),
+        ("tl", 32, "uint16"), ("labu nbu xo", 256, "uint16"),
+        ("k0 lab32 key kt ks y1 d1", 256, "float32"),
+        ("ldt ndt old thr up nu cand cm dnew y2 d2", 256, "bfloat16"),
+        ("w0 w1 w2 w3", WW, "bfloat16"), ("fr0 fr1 fr2", 384, "float32")):
+    for name in names.split():
+        SCRATCH[name] = ("sbuf", [128, width], kind)
+
+SEMAPHORES = (["qv", "qs", "qp", "qg", "alst"] + ["aw%d" % t for t in range(RO)] + ["af%d" % t for t in range(RO - 1)]
+              + ["dm%d" % i for i in range(40)] + ["rm%d" % i for i in range(24)])
+
+
+def rank_program(g, core, T, topo):
+    rank = T.rank_of(core)
+    if rank is None:
+        return
+    Q = {"v": g.vector, "s": g.scalar, "p": g.tensor, "g": g, "y": g.sync}
+    ops, lastw, readers = [], {}, {}
+    cnt = {"dm": 0, "rm": 0}
+
+    def add(q, kind, fn, rd, wr, sem=None, val=0):
+        o = {"q": q, "kind": kind, "fn": fn, "sem": sem, "val": val, "need": False, "deps": []}
+        dep = []
+        for r in rd:
+            if r in lastw:
+                dep.append(lastw[r])
+        for w in wr:
+            for x in ([lastw[w]] if w in lastw else []) + readers.get(w, []):
+                if not (q == "p" and x["q"] == q):
+                    dep.append(x)
+        for x in dep:
+            if all(x is not z for z in o["deps"]):
+                o["deps"].append(x)
+                x["need"] = True
+        for r in rd:
+            readers.setdefault(r, []).append(o)
+        for w in wr:
+            lastw[w] = o
+            readers[w] = []
+        ops.append(o)
+
+    def comp(q, fn, rd, wr):
+        add(q, "c", fn, rd, wr, "q" + q)
+
+    def dma(q, out, in_, rd, wr):
+        s = "dm%d" % cnt["dm"]
+        cnt["dm"] += 1
+        add(q, "d", lambda: Q[q].dma_start(out, in_).then_inc(T.sem[s], 16), rd, wr, s, 16)
+
+    def arrival(sem, val, wr):
+        add(None, "a", None, [], wr, sem, val)
+
+    def peer(d):
+        return T.cores[(rank + d) % N]
+
+    def bits(dst, lo, hi):
+        m = 0
+        for e in topo.engines(core, dst)[lo:hi]:
+            m |= 1 << e
+        return m
+
+    ne = len(topo.engines(core, peer(1)))
+
+    def send(parts, rsem, rd):
+        s = "rm%d" % cnt["rm"]
+        cnt["rm"] += 1
+
+        def fn():
+            if len(parts) == 1 and len(parts[0][3]) == 1:
+                dst, lo, hi, srcs, out = parts[0]
+                rid, pid = topo.addr(dst)[0:2]
+                g.remote_dma(out, srcs[0], T.sem[rsem], T.sem[s], pid, rid, bits(dst, lo, hi))
+                return
+            tr = []
+            for dst, lo, hi, srcs, out in parts:
+                rid, pid = topo.addr(dst)[0:2]
+                tr.append(RemoteDMATransfer(dst_ids=[DstId(rid=rid, pnc=pid)], dma_engine_mask=bits(dst, lo, hi),
+                                            remote_sem=T.sem[rsem], srcs=list(srcs), dsts=[out],
+                                            alu_op=2 if len(srcs) > 1 else 0))
+            g.remote_dma_fused(tr, local_sem=T.sem[s])
+        add("g", "r", fn, rd, [], s, sum(p[2] - p[1] for p in parts))
+
+    vec, act, pe = g.vector, g.scalar, g.tensor
+
+    def ts(out, in0, s1, s2, op0, op1, rd, wr):
+        if op1 is None:
+            comp("v", lambda: vec.tensor_scalar(out, in0, s1, None, op0), rd, wr)
+        else:
+            comp("v", lambda: vec.tensor_scalar(out, in0, s1, s2, op0, op1), rd, wr)
+
+    def tt(out, in0, in1, op, rd, wr):
+        comp("v", lambda: vec.tensor_tensor(out, in0, in1, op), rd, wr)
+
+    def cp(out, in_, rd, wr):
+        comp("v", lambda: vec.tensor_copy(out, in_), rd, wr)
+
+    def ms(ap, const, wr):
+        comp("v", lambda: vec.memset(ap, const), [], wr)
+
+    def tr32(out, in_, rd, wr):
+        comp("v", lambda: vec.transpose(out, in_), rd, wr)
+
+    def scan(out, d0, d1, op0, op1, rd, wr):
+        comp("v", lambda: vec.tensor_tensor_scan(out, d0, d1, 0.0, op0, op1), rd, wr)
+
+    def ac(out, in_, func, rd, wr, **kw):
+        comp("s", lambda: act.activation(out, in_, func, **kw), rd, wr)
+
+    def iota(out, pat, base, cm, wr, flt=True):
+        if flt:
+            comp("g", lambda: g.iota(out, pat, base, cm, allow_small_or_imprecise_dtypes=True), [], wr)
+        else:
+            comp("g", lambda: g.iota(out, pat, base, cm), [], wr)
+
+    def mms(lst, rd, wr):
+        def fn():
+            r = None
+            for out, l, rh, a, b in lst:
+                r = pe.matmul(out, l, rh, a, b)
+            return r
+        comp("p", fn, rd, wr)
+
+    W = [T["w%d" % t] for t in range(RO)]
+    ps = T.ps
+
+    def mat(j):
+        return T.mat[:, 128 * j:128 * (j + 1)]
+    ALLM = ["mat%d" % j for j in range(NMAT)]
+    PM, GAM, KC, GB, C48 = [T.col[:, j:j + 1] for j in range(5)]
+
+    dma("s", T.fli[:], T.fl[:], [], ["fli"])
+    dma("y", W[0][:, PAD:TW], T.d0[:], [], ["w0own"])
+    dma("s", T.sni[:], T.snd[:], [], ["sni"])
+    dma("y", T.labi[:, PAD:TW], T.lab[:], [], ["labi"])
+    dma("y", T.ldw[:, PAD:TW], T.ld[:], [], ["ldw"])
+    dma("y", W[0][:, PAD + 3072:PAD + 3088], T.rt[:], [], ["w0rt"])
+    dma("y", T.nbw[:, PAD:TW], T.nb[:], [], ["nbw"])
+    dma("y", T.ndw[:, PAD:TW], T.nd[:], [], ["ndw"])
+    for t in range(RO):
+        arrival("aw%d" % t, 3 * ne, ["w%dg" % t])
+    for t in range(RO - 1):
+        arrival("af%d" % t, 2 * ne, ["fr%d" % t])
+    arrival("alst", ne, ["lst"])
+
+    iota(T.pidx[:], [[0, 1]], 0, 1, ["pidx"], False)
+    iota(T.va[:], [[-16, 8], [0, 16]], 0, 1, ["va"])
+    iota(T.vb[:], [[1, 128]], 0, -1, ["vb"])
+    iota(T.dumc[:], [[0, 2], [1, 48]], 1600, 0, ["dumc"])
+    iota(T.ci[:], [[1, 16]], 0, 0, ["ci"])
+    iota(T.cv[:, 0:272], [[1, 272]], 0, 0, ["cv"])
+    iota(T.vals[:, 0:768], [[1, 48], [96, 16]], PAD, 0, ["valsv"])
+    iota(T.vals[:, 768:V], [[1, 48], [96, 16]], PAD + 48, 0, ["valss"])
+
+    ms(T.mx[:], 0.0, ["mx"])
+    ac(T.cs[:, 0:272], T.mx[:], F.Silu, ["mx"], ["cs"])
+    ms(W[0][:, 0:PAD], 255.0, ["w0pad"])
+    ms(T.ldw[:, 0:PAD], 255.0, ["ldpad"])
+    ms(T.ndw[:, 0:PAD], 255.0, ["ndpad"])
+    ts(T.pmi[:], T.pidx[:], 15, None, A.bitwise_and, None, ["pidx"], ["pmi"])
+    ts(T.gmi[:], T.pidx[:], 16, None, A.bitwise_and, None, ["pidx"], ["gmi"])
+    ts(T.ta[:], T.va[:], 0.0, None, A.is_ge, None, ["va"], ["ta"])
+    cp(PM, T.pmi[:], ["pmi"], ["pm"])
+    ts(C48, T.pmi[:], 48.0, None, A.mult, None, ["pmi"], ["c48"])
+    ts(GAM, T.gmi[:], -1.0, None, A.add, None, ["gmi"], ["gam"])
+    ts(T.tb[:], T.vb[:], 0.0, None, A.is_gt, None, ["vb"], ["tb"])
+    ts(T.tc[:], T.va[:], 15.0, None, A.is_le, None, ["va"], ["tc"])
+    tt(T.lt[:], T.ta[:], T.tb[:], A.mult, ["ta", "tb"], ["lt"])
+    tt(T.blk[:], T.ta[:], T.tc[:], A.mult, ["ta", "tc"], ["blk"])
+    ts(T.dum[:], T.dumc[:], C48, None, A.add, None, ["dumc", "c48"], ["dum"])
+    ts(T.eq[:], T.ci[:], PM, None, A.is_equal, None, ["ci", "pm"], ["eq"])
+    ts(GB, PM, 32.0, GAM, A.mult, A.add, ["pm", "gam"], ["gb"])
+    tt(T.wt[:, 1:16], T.eq[:, 0:15], T.eq[:, 1:16], A.subtract, ["eq"], ["wt"])
+    ts(T.wt[:, 0:1], T.eq[:, 15:16], 8.0, None, A.mult, None, ["eq"], ["wt0"])
+    cp(T.snu[:], T.sni[:], ["sni"], ["snu"])
+    NS = 7
+    for j in range(NS):
+        ac(mat(j), T.blk[:], F.Identity, ["blk", "wt", "wt0"], ["mat%d" % j], scale=T.wt[:, j:j + 1])
+
+    def late_constants():
+        ts(T.gl[:], T.ci[:], GB, 1.0, A.add, A.add, ["ci", "gb"], ["gl"])
+        ms(T.labi[:, 0:PAD], NP - 1, ["labpad"])
+        ms(T.nbw[:, 0:PAD], NP - 1, ["nbpad"])
+        ms(W[0][:, PAD + 3088:WW], 255.0, ["w0none"])
+        for j in range(NS, 16):
+            ts(mat(j), T.blk[:], T.wt[:, j:j + 1], None, A.mult, None, ["blk", "wt"], ["mat%d" % j])
+        for j in range(16, 21):
+            ts(mat(j), T.blk[:], T.eq[:, j - 5:j - 4], None, A.mult, None, ["blk", "eq"], ["mat%d" % j])
+        ts(mat(21), T.blk[:], -4096.0, None, A.mult, None, ["blk"], ["mat21"])
+
+    def slot_lists():
+        ts(T.sa[:], T.sni[:], -47.5, 1.0 / 96.0, A.add, A.mult, ["sni"], ["sa"])
+        ts(KC, PM, -8.0, None, A.add, None, ["pm"], ["kc"])
+        cp(T.sb[:], T.sa[:], ["sa"], ["sb"])
+        ms(T.r2[:], 3328.0, ["r2"])
+        ts(T.sc[:], T.sb[:], 96.0, None, A.mult, None, ["sb"], ["sc"])
+        ms(T.k0[:], 0.0, ["k0"])
+        tt(T.sd[:], T.sc[:], T.sni[:], A.add, ["sc", "sni"], ["sd"])
+        ms(T.y1[:], 0.0, ["y1"])
+        cp(T.su[:, 0:96], T.sd[:], ["sd"], ["su0"])
+        ts(T.su[:, 96:192], T.sd[:], 96.0, None, A.add, None, ["sd"], ["su1"])
+        q = ne // 4
+        send([(peer(1), 0, q, [T.su[:, 0:32]], T.lst[:, 0:32]), (peer(2), q, 2 * q, [T.su[:, 128:160]], T.lst[:, 32:64]),
+              (peer(3), 2 * q, 3 * q, [T.su[:, 64:96]], T.lst[:, 64:96]),
+              (peer(3), 3 * q, 4 * q, [T.su[:, 160:192]], T.lst[:, 96:128])], "alst", ["su0", "su1"])
+        ms(T.y2[:], 0.0, ["y2"])
+        ms(T.k0[:, 0:256:16], 20000.0, ["k0"])
+
+    def send_d(src, dstw):
+        for d in range(1, N):
+            a = GS * (d - 1)
+            ac(T.sbf[:, a:a + GS], W[src][:, PAD:TW].indirect(T.snu[:, 32 * (d - 1):32 * d]), F.Identity,
+               ["w%down" % src, "snu"], ["sbf%d" % d])
+            send([(peer(d), 0, ne, [T.sbf[:, a:a + GS]], W[dstw][:, TW + a:TW + a + GS])], "aw%d" % dstw, ["sbf%d" % d])
+
+    send_d(0, 0)
+    iota(T.gs[:, V:2 * V], [[0, V]], 0, 0, ["gs"])
+    dma("y", T.gv[0:128:16, 0:V], T.gs[0:128:16, V:2 * V], ["gs"], ["gvown"])
+    dma("y", T.ov[0:128:16, :], T.gs[0:128:8, V:2 * V], ["gs"], ["ov"])
+    dma("y", T.ow[0:128:16, :], T.gs[0:128:8, V:2 * V], ["gs"], ["ow"])
+    dma("y", T.gs[0:128:16, 0:V], T.gs[0:128:16, V:2 * V], ["gs"], ["gsown"])
+
+    for t in range(RO):
+        last = t == RO - 1
+        c = 12 + t
+        wn = "w%d" % t
+        wown = [wn + "own", wn + "pad"]
+        wall = [wn + "own", wn + "g", wn + "rt", wn + "none"]
+        if t == 0:
+            raw, rn, th = T.fli[:], "fli", 0.5
+        else:
+            R = T["fr%d" % (t - 1)]
+            tt(T.x2[:], R[:, 0:192], R[:, 192:384], A.max, ["fr%d" % (t - 1), "oc%d" % (t - 1)], ["x2"])
+            tt(T.raw[:], T.x2[:, 0:96], T.x2[:, 96:192], A.max, ["x2"], ["raw"])
+            raw, rn, th = T.raw[:], "raw", 100.0 * t - 50.0
+        ts(T.fg[:], raw, th, None, A.is_ge, None, [rn], ["fg"])
+        ts(T.fb[:], raw, th, 8192.0, A.is_ge, A.mult, [rn], ["fb"])
+        scan(T.pl[:], T.fg[:], T.fg[:], A.add, A.max, ["fg"], ["pl"])
+        ex = ps[:, 7 * 512 + 256:7 * 512 + 257]
+        mms([(ex, T.lt[:], T.pl[:, 95:96], True, True)], ["lt", "pl"], ["b7"])
+        tt(T.yy[:], T.dum[:], T.fb[:], A.subtract, ["dum", "fb"], ["yy"])
+        tt(T.xx[:], T.pl[:], T.yy[:], A.max, ["pl", "yy"], ["xx"])
+        ts(T.off[:], T.xx[:], ex, GAM, A.add, A.add, ["xx", "b7", "gam"], ["off"])
+        cp(T.cv[:].indirect(T.off[:, 0:48]), T.vals[:, 0:768], ["off", "valsv", "cv"], ["cv"])
+        ac(T.cs[:].indirect(T.off[:, 48:96]), T.vals[:, 768:V], F.Silu, ["off", "valss", "cs"], ["cs"])
+        if t == 0:
+            late_constants()
+        tt(T.mx[:], T.cv[:, 0:272], T.cs[:, 0:272], A.max, ["cv", "cs"], ["mx"])
+        tr32(T.tt[:, 0:256], T.mx[:, 0:256], ["mx"], ["tt0"])
+        tr32(T.tt[:, 256:512], T.mx[:, 16:272], ["mx"], ["tt1"])
+        ts(T.tl[:], T.tt[:].indirect(T.gl[:, 0:2]), 0.25, None, A.add, None, ["tt0", "tt1", "gl"], ["tl"])
+        L = T.tl[:, 0:16]
+        ac(T.ldt[:], T.ldw[:].indirect(L), F.Identity, ["ldw", "ldpad", "tl"], ["ldt"])
+        if t == 0:
+            cp(T.labu[:], T.labi[:].indirect(L), ["labi", "labpad", "tl"], ["labu"])
+            slot_lists()
+        else:
+            cp(T.labu[:], T.labf[:].indirect(L), ["labf", "tl"], ["labu"])
+        if not last:
+            iota(T.cv[:, 0:272], [[1, 272]], 0, 0, ["cv"])
+            iota(T.cs[:, 0:272], [[0, 272]], 0, 0, ["cs"])
+        if t == 0:
+            iota(T.r1[:], [[1, 272]], -224, 0, ["r1"])
+            iota(T.st[:], [[100, 3], [0, 256]], 100, 0, ["st"])
+            iota(T.gv[:, V:2 * V], [[0, V]], 0, 0, ["gv"])
+            comp("g", lambda: g.affine_select(T.labf[:], T.labi[:], [[0, TW]], A.is_ge, 0.0, 1, 0),
+                 ["labi", "labpad"], ["labf"])
+        win = W[t][:, PAD:PAD + NP]
+
+        def gather(q, u0, u1):
+            lu, nm = (T.labu, "labu") if u0 < 8 else (T.nbu, "nbu")
+            o = lu[:, 32 * (u0 % 8):32 * (u0 % 8) + 32 * (u1 - u0)]
+            out = T.gt[:, 512 * u0:512 * u1]
+            wr = ["gt%d" % u for u in range(u0, u1)]
+            if q == "v":
+                cp(out, win.indirect(o), wall + [nm], wr)
+            else:
+                ac(out, win.indirect(o), F.Identity, wall + [nm], wr)
+
+        def diffs(u):
+            b = u % 6
+            a = 32 * (u % 8)
+            lst = [(ps[:, 512 * b:512 * b + 512:16], mat(0), T.ldt[:, a:a + 32], True, True)]
+            for i in range(1, 16):
+                out = ps[:, 512 * b + i:512 * b + 512:16]
+                if u >= 8:
+                    lst.append((out, mat(i), T.ndt[:, a:a + 32], True, True))
+                elif i == c:
+                    lst.append((out, mat(16 + c - 12), T.ldt[:, a:a + 32], True, True))
+                elif i < c or b >= 4 or (t == 0 and u < 6):
+                    lst.append((out, mat(i), T.ldt[:, a:a + 32], True, True))
+            mms(lst, ALLM + ["ldt"] + (["ndt"] if u >= 8 else []), ["b%d" % b])
+
+        def least(u0, u1):
+            b = u0 % 6
+            scan(T.sn[:, 512 * u0:512 * u1], ps[:, 512 * b:512 * (b + u1 - u0)], T.gt[:, 512 * u0:512 * u1], A.add, A.min,
+                 ["b%d" % (u % 6) for u in range(u0, u1)] + ["gt%d" % u for u in range(u0, u1)],
+                 ["sn%d" % u for u in range(u0, u1)])
+
+        for u in range(6):
+            diffs(u)
+        gather("s", 2, 4)
+        gather("v", 0, 2)
+        cp(T.nbu[:], T.nbw[:].indirect(L), ["nbw", "nbpad", "tl"], ["nbu"])
+        ac(T.ndt[:], T.ndw[:].indirect(L), F.Identity, ["ndw", "ndpad", "tl"], ["ndt"])
+        gather("s", 4, 6)
+        gather("s", 6, 8)
+        least(0, 2)
+        diffs(6)
+        diffs(7)
+        least(2, 4)
+        n15 = ps[:, 6 * 512:6 * 512 + 256]
+        mms([(n15, mat(20), T.ndt[:], True, True)], ["mat20", "ndt"], ["b6"])
+        diffs(8)
+        diffs(9)
+        cp(T.old[:], W[t][:, 0:TW].indirect(L), wown + ["tl"], ["old"])
+        least(4, 6)
+        diffs(10)
+        diffs(11)
+        gather("s", 8, 10)
+        gather("s", 10, 12)
+        gather("s", 12, 14)
+        gather("s", 14, 15)
+        gather("s", 15, 16)
+        if not last:
+            ac(T.nb32[:], T.nbw[:].indirect(T.tl[:, 0:17]), F.Identity, ["nbw", "nbpad", "tl"], ["nb32"])
+        ac(T.lab32[:], T.labf[:].indirect(L), F.Identity, ["labf", "tl"], ["lab32"])
+        least(6, 8)
+        diffs(12)
+        diffs(13)
+        th2 = ps[:, 7 * 512:7 * 512 + 256]
+        tt(T.thr[:], T.sn[:, c:4096:16], T.old[:], A.min, ["sn%d" % u for u in range(8)] + ["old"], ["thr"])
+        least(8, 10)
+        diffs(14)
+        diffs(15)
+        tt(th2, T.thr[:], n15, A.subtract, ["thr", "b6"], ["b7"])
+        if last:
+            ms(T.y1[:, c - 1:256:16], 0.0, ["y1"])
+        least(10, 12)
+        za, zb, zw = ps[:, 2304:2560], ps[:, 2560:2576], ps[:, 2304:2576]
+        if not last:
+            mms([(za, mat(20), T.r2[:, 0:256], True, False), (za, mat(20), T.r1[:, 0:256], False, False),
+                 (zb, mat(20), T.r2[:, 256:272], True, False), (zb, mat(20), T.r1[:, 256:272], False, False)],
+                ["mat20", "r1", "r2"], ["b4", "b5"])
+        least(12, 14)
+        least(14, 15)
+        least(15, 16)
+        sc = T.sn[:, 4096 + 15:8192:16]
+        scn = ["sn%d" % u for u in range(8, 16)]
+        tt(T.up[:], sc, th2, A.is_lt, scn + ["b7"], ["up"])
+        ac(T.nu[:], T.up[:], F.Identity, ["up"], ["nu"], scale=-512.0, bias=512.0)
+        tt(T.cand[:], sc, n15, A.add, scn + ["b6"], ["cand"])
+
+        def new_d(step):
+            if step == 0:
+                tt(T.cm[:], T.cand[:], T.nu[:], A.max, ["cand", "nu"], ["cm"])
+            if step == 1:
+                tt(T.dnew[:], T.cm[:], T.old[:], A.min, ["cm", "old"], ["dnew"])
+            if step == 2:
+                cp(W[t][:, 0:TW].indirect(L), T.dnew[:], ["dnew", "tl"], wown)
+
+        def new_labels(fill):
+            if last:
+                ac(T.key[:], T.cm[:], F.Identity, ["cm", "kc"], ["key"], scale=32.0, bias=KC)
+            else:
+                ts(T.key[:], T.cm[:], 32.0, KC, A.mult, A.add, ["cm", "kc"], ["key"])
+            fill(0)
+            tr32(T.kt[:], T.key[:], ["key"], ["kt"])
+            fill(1)
+            scan(T.ks[:], T.k0[:], T.kt[:], A.add, A.min, ["k0", "kt"], ["ks"])
+            fill(2)
+            ts(T.q1[:], T.ks[:, 15:256:16], 8168.0, 1.0 / 32.0, A.min, A.mult, ["ks"], ["q1"])
+            if t > 0 and not last:
+                ms(T.y1[:, c - 1:256:16], 0.0, ["y1"])
+            cp(T.li[:], T.q1[:], ["q1"], ["li"])
+            if t > 0 and not last:
+                ms(T.y2[:, c - 1:256:16], 0.0, ["y2"])
+            tt(T.df[:], T.q1[:], T.li[:], A.subtract, ["q1", "li"], ["df"])
+            if not last:
+                ts(T.y2[:, c:256:16], T.li[:], -255.0, None, A.add, None, ["li"], ["y2"])
+            ts(T.y1[:, c:256:16], T.df[:], 32.0, -8.0, A.mult, A.add, ["df"], ["y1"])
+            if not last:
+                tr32(T.d2[:], T.y2[:], ["y2"], ["d2"])
+            tr32(T.d1[:], T.y1[:], ["y1"], ["d1"])
+            if not last:
+                tt(T.ldw[:].indirect(L), T.ldt[:], T.d2[:], A.add, ["ldt", "d2", "tl"], ["ldw", "ldpad"])
+            tt(T.labf[:].indirect(L), T.lab32[:], T.d1[:], A.add, ["lab32", "d1", "tl"], ["labf"])
+
+        if last:
+            def tail(step):
+                if step == 0:
+                    new_d(1)
+                    new_d(2)
+                    dma("y", T.yd[:], W[t][:, PAD:TW], [wn + "own"], ["yd"])
+            new_d(0)
+            new_labels(tail)
+            dma("y", T.yl[15:128:16, :], T.labf[15:128:16, PAD:TW], ["labf"], ["yl"])
+            break
+        mms([(za, mat(21), T.up[:], False, True), (zb, mat(21), T.up[:, 0:16], False, True)], ["mat21", "up"], ["b4", "b5"])
+        tt(T.zz[:], T.nb32[:], zw, A.max, ["nb32", "b4", "b5"], ["zz"])
+        tr32(T.tt[:, 0:256], T.zz[:, 0:256], ["zz"], ["tt0"])
+        tr32(T.tt[:, 256:512], T.zz[:, 16:272], ["zz"], ["tt1"])
+        cp(T.xo[:, 0:160], T.tt[:].indirect(T.gl[:, 0:10]), ["tt0", "tt1", "gl"], ["xo0"])
+        cp(T.xo[:, 160:256], T.tt[:].indirect(T.gl[:, 10:16]), ["tt0", "tt1", "gl"], ["xo1"])
+        stamp = T.st[:, 256 * t:256 * (t + 1)]
+        for i in range(9):
+            ac(T.gs[:].indirect(T.xo[:, 16 * i:16 * i + 16]), stamp, F.Silu, ["xo0", "st"], ["gs", "gsown"])
+        for i in range(9, 16):
+            cp(T.gv[:].indirect(T.xo[:, 16 * i:16 * i + 16]), stamp, ["xo0" if i < 10 else "xo1", "st"], ["gv", "gvown"])
+            new_d(i - 9)
+        dma("y", W[t + 1][:, 0:TW], W[t][:, 0:TW], wown, ["w%down" % (t + 1), "w%dpad" % (t + 1)])
+        dma("y", T.ev[:], T.gv[0:128:16, 0:V], ["gv"], ["ev"])
+        dma("y", T.es[:], T.gs[0:128:16, 0:V], ["gs"], ["es"])
+        tt(T.ov[:].indirect(T.lst[:, 0:64]), T.gv[:, V:V + 2 * GS], T.gs[:, V:V + 2 * GS], A.max, ["lst", "gv", "gs"], ["ov"])
+        ac(T.ow[:].indirect(T.lst[:, 64:96]), T.gs[:, V + 2 * GS:2 * V], F.Silu, ["lst", "gs"], ["ow"])
+        ac(T.ow[:].indirect(T.lst[:, 96:128]), T.gv[:, V + 2 * GS:2 * V], F.Silu, ["lst", "gv"], ["ow"])
+        dma("y", T.xv[:], T.ov[0:128:16, :], ["ov"], ["xv"])
+        dma("s", T.xs[:], T.ow[0:128:16, :], ["ow"], ["xs"])
+        R = T["fr%d" % t]
+        h = ne // 2
+        send([(peer(-1), 0, h, [T.xv[:, 0:96]], R[:, 0:96]), (peer(-2), h, ne, [T.xv[:, 96:192]], R[:, 96:192])],
+             "af%d" % t, ["xv"])
+        send([(peer(-3), 0, ne, [T.xs[:, 0:96], T.xs[:, 96:192]], R[:, 192:288])], "af%d" % t, ["xs"])
+        send_d(t, t + 1)
+        ac(W[t + 1][:, PAD + 3072:WW], W[0][:, PAD + 3072:WW], F.Identity, ["w0rt", "w0none"],
+           ["w%drt" % (t + 1), "w%dnone" % (t + 1)])
+        ts(T.beyond[:], T.pl[:], ex, 256.0, A.add, A.is_gt, ["pl", "b7"], ["beyond"])
+
+        def own_flags(step):
+            if step == 0:
+                tt(T.rem[:], T.beyond[:], T.fb[:], A.mult, ["beyond", "fb"], ["rem"])
+            if step == 1:
+                tt(T.oc[:], T.ev[:], T.rem[:], A.max, ["ev", "rem"], ["oc"])
+            if step == 2:
+                tt(R[:, 288:384], T.oc[:], T.es[:], A.max, ["oc", "es"], ["oc%d" % t])
+        new_labels(own_flags)
+        if t == RO - 2:
+            dma("y", T.yl[:], T.labf[:, PAD:TW], ["labf", "w%dg" % (t + 1)], ["yl"])
+
+    num = {}
+    for o in ops:
+        if o["kind"] == "c" and o["need"]:
+            num[o["sem"]] = num.get(o["sem"], 0) + 1
+            o["val"] = num[o["sem"]]
+    seen, anyq = {}, {}
+    for o in ops:
+        if o["kind"] == "a":
+            continue
+        q = o["q"]
+        want = {}
+        for x in o["deps"]:
+            want[x["sem"]] = max(want.get(x["sem"], 0), x["val"])
+        for s in want:
+            if seen.get((q, s), 0) < want[s]:
+                Q[q].wait_ge(T.sem[s], want[s])
+                seen[(q, s)] = want[s]
+                anyq[s] = max(anyq.get(s, 0), want[s])
+        r = o["fn"]()
+        if o["kind"] == "c" and o["need"]:
+            r.then_inc(T.sem[o["sem"]], 1)
+    for o in ops:
+        if o["kind"] != "c" and anyq.get(o["sem"], 0) < o["val"]:
+            g.wait_ge(T.sem[o["sem"]], o["val"])

@@ -4,34 +4,38 @@ from concourse.mybir import AluOpType, ActivationFunctionType
 A = AluOpType
 F = ActivationFunctionType
 N, V, GS, CAP, RO = 4, 1536, 512, 256, 4
-PAD = 288
 NP = V + 3 * GS + 17
-WW = PAD + 3104
-TW = PAD + V
-CW = 3920
+WW = 3104
+TW = V + CAP
+NC = TW // 16
+HW = 3840
 GW = 3376
-NMAT = 22
+STAMP = (32.0, 256.0, 2048.0)
+ROUND = 1.5 * 2.0 ** 23
+XV, CUTS, LAST = 1, (20, 24, 28, 30, 31), (30, 31)
+MATS = ["d%d" % i for i in range(1, 16)] + "l14 l15 n15 one neg p512 n512 kd sum4k tri e15 blk trs".split()
 
 SCRATCH = {"ps": ("psum", [128, 4096], "float32")}
 for names, width, kind in (
-        ("nbw labi", TW, "int32"), ("labf", TW, "float32"), ("ndw ldw", TW, "bfloat16"),
-        ("fli sni sb sc sd", 96, "int32"), ("snu off", 96, "uint16"), ("su", 192, "uint16"), ("lst", 128, "uint16"),
-        ("sa dumc dum raw fb yy xx beyond rem oc ev es", 96, "float32"), ("fg pl", 96, "bfloat16"),
-        ("x2 xv xs", 192, "float32"),
-        ("cv cs", CW, "float32"), ("vals", V, "float32"), ("gv gs", GW, "float32"), ("ov ow", 3072, "float32"),
-        ("gt sn", 8192, "bfloat16"), ("sbf", V, "bfloat16"), ("mat", NMAT * 128, "bfloat16"),
-        ("pidx pmi gmi", 1, "int32"), ("col", 8, "float32"), ("ci eq wt q1 df", 16, "float32"), ("li", 16, "int32"),
-        ("gl", 16, "uint16"), ("va vb ta tb tc", 128, "float32"), ("blk lt", 128, "bfloat16"),
-        ("r1 r2", 272, "bfloat16"), ("st", 768, "float32"), ("mx zz nb32", 272, "float32"), ("tt", 512, "float32"),
-        ("tl", 32, "uint16"), ("labu nbu xo", 256, "uint16"),
-        ("k0 lab32 key kt ks y1 d1", 256, "float32"),
-        ("ldt ndt old thr up nu cand cm dnew y2 d2", 256, "bfloat16"),
+        ("nbw labi", TW, "int32"), ("labf lo", TW, "float32"), ("ndw ldw", TW, "bfloat16"),
+        ("fli", V, "int32"), ("flb sbf", V, "bfloat16"), ("sni sr sa sb sc sd", 96, "int32"), ("snu lst", 96, "uint16"),
+        ("off", 8, "uint16"), ("vi vj", NC, "int32"),
+        ("rem two", 96, "float32"), ("xf", 384, "float32"), ("fx", 2 * NC, "bfloat16"), ("crow cis", NC, "bfloat16"),
+        ("hw", HW, "bfloat16"), ("gv gs", GW, "float32"), ("ov ow", 3072, "float32"),
+        ("gt sn", 8192, "bfloat16"), ("mat", len(MATS) * 128, "bfloat16"),
+        ("vc vd b2 b3", 144, "float32"), ("o1 o2 b8", 144, "bfloat16"), ("gx idf ta tb", 128, "float32"),
+        ("pidx pmi gmi ggi", 1, "int32"), ("col", 16, "float32"), ("ci eq wt df ya yb yc", 16, "float32"),
+        ("dua", 16, "bfloat16"), ("gl", 16, "uint16"), ("tl", 16, "uint16"),
+        ("r1 r2", 272, "bfloat16"), ("st", 768, "float32"), ("zz nb32", 272, "float32"), ("tt", 512, "float32"),
+        ("labu nbu xo", 256, "uint16"), ("k0 lab32 kt ks y1 d1", 256, "float32"),
+        ("ldt ndt up dm y2 d2 dec hg hm ones", 256, "bfloat16"),
         ("w0 w1 w2 w3", WW, "bfloat16"), ("fr0 fr1 fr2", 384, "float32")):
     for name in names.split():
         SCRATCH[name] = ("sbuf", [128, width], kind)
 
-SEMAPHORES = (["qv", "qs", "qp", "qg", "alst"] + ["aw%d" % t for t in range(RO)] + ["af%d" % t for t in range(RO - 1)]
-              + ["dm%d" % i for i in range(40)] + ["rm%d" % i for i in range(24)])
+SEMAPHORES = (["qv", "qs", "qp", "qg", "alst"] + ["aw%d" % t for t in range(RO)]
+              + ["af%d%d" % (t, h) for t in range(RO - 1) for h in range(2)]
+              + ["dm%d" % i for i in range(48)] + ["rm%d" % i for i in range(24)])
 
 
 def rank_program(g, core, T, topo):
@@ -48,6 +52,8 @@ def rank_program(g, core, T, topo):
         for r in rd:
             if r in lastw:
                 dep.append(lastw[r])
+            if r[0] == "#":
+                dep += [x for x in readers.get(r, []) if x["q"] != q]
         for w in wr:
             for x in ([lastw[w]] if w in lastw else []) + readers.get(w, []):
                 if not (q == "p" and x["q"] == q):
@@ -66,10 +72,17 @@ def rank_program(g, core, T, topo):
     def comp(q, fn, rd, wr):
         add(q, "c", fn, rd, wr, "q" + q)
 
-    def dma(q, out, in_, rd, wr):
+    def dmas(q, pairs, rd, wr):
         s = "dm%d" % cnt["dm"]
         cnt["dm"] += 1
-        add(q, "d", lambda: Q[q].dma_start(out, in_).then_inc(T.sem[s], 16), rd, wr, s, 16)
+
+        def fn():
+            for out, in_ in pairs:
+                Q[q].dma_start(out, in_).then_inc(T.sem[s], 16)
+        add(q, "d", fn, rd, wr, s, 16 * len(pairs))
+
+    def dma(q, out, in_, rd, wr):
+        dmas(q, [(out, in_)], rd, wr)
 
     def arrival(sem, val, wr):
         add(None, "a", None, [], wr, sem, val)
@@ -84,23 +97,23 @@ def rank_program(g, core, T, topo):
         return m
 
     ne = len(topo.engines(core, peer(1)))
+    q4 = ne // 4
 
     def send(parts, rsem, rd):
         s = "rm%d" % cnt["rm"]
         cnt["rm"] += 1
 
         def fn():
-            if len(parts) == 1 and len(parts[0][3]) == 1:
-                dst, lo, hi, srcs, out = parts[0]
+            if len(parts) == 1:
+                dst, lo, hi, src, out = parts[0]
                 rid, pid = topo.addr(dst)[0:2]
-                g.remote_dma(out, srcs[0], T.sem[rsem], T.sem[s], pid, rid, bits(dst, lo, hi))
+                g.remote_dma(out, src, T.sem[rsem], T.sem[s], pid, rid, bits(dst, lo, hi))
                 return
             tr = []
-            for dst, lo, hi, srcs, out in parts:
+            for dst, lo, hi, src, out in parts:
                 rid, pid = topo.addr(dst)[0:2]
                 tr.append(RemoteDMATransfer(dst_ids=[DstId(rid=rid, pnc=pid)], dma_engine_mask=bits(dst, lo, hi),
-                                            remote_sem=T.sem[rsem], srcs=list(srcs), dsts=[out],
-                                            alu_op=2 if len(srcs) > 1 else 0))
+                                            remote_sem=T.sem[rsem], srcs=[src], dsts=[out], alu_op=0))
             g.remote_dma_fused(tr, local_sem=T.sem[s])
         add("g", "r", fn, rd, [], s, sum(p[2] - p[1] for p in parts))
 
@@ -124,8 +137,8 @@ def rank_program(g, core, T, topo):
     def tr32(out, in_, rd, wr):
         comp("v", lambda: vec.transpose(out, in_), rd, wr)
 
-    def scan(out, d0, d1, op0, op1, rd, wr):
-        comp("v", lambda: vec.tensor_tensor_scan(out, d0, d1, 0.0, op0, op1), rd, wr)
+    def scan(out, d0, d1, op0, op1, rd, wr, first=0.0):
+        comp("v", lambda: vec.tensor_tensor_scan(out, d0, d1, first, op0, op1), rd, wr)
 
     def ac(out, in_, func, rd, wr, **kw):
         comp("s", lambda: act.activation(out, in_, func, **kw), rd, wr)
@@ -136,165 +149,218 @@ def rank_program(g, core, T, topo):
         else:
             comp("g", lambda: g.iota(out, pat, base, cm), [], wr)
 
+    def fill(out, width, value, wr, flt=True):
+        iota(out, [[0, width]], int(value), 0, wr, flt)
+
     def mms(lst, rd, wr):
         def fn():
             r = None
-            for out, l, rh, a, b in lst:
-                r = pe.matmul(out, l, rh, a, b)
+            for j, m in enumerate(lst):
+                a, b = m[3:5] if len(m) > 3 else (j == 0, j == len(lst) - 1)
+                r = pe.matmul(m[0], m[1], m[2], a, b)
             return r
         comp("p", fn, rd, wr)
 
     W = [T["w%d" % t] for t in range(RO)]
     ps = T.ps
 
-    def mat(j):
+    def mat(name):
+        j = MATS.index(name)
         return T.mat[:, 128 * j:128 * (j + 1)]
-    ALLM = ["mat%d" % j for j in range(NMAT)]
-    PM, GAM, KC, GB, C48 = [T.col[:, j:j + 1] for j in range(5)]
 
-    dma("s", T.fli[:], T.fl[:], [], ["fli"])
-    dma("y", W[0][:, PAD:TW], T.d0[:], [], ["w0own"])
+    def lane(buf, l, rows=128):
+        return buf[0:rows, 16 - l:144 - l]
+
+    PM, GP, GB, KD, E15, WL, MINS, DEC, VOFF, GM = [T.col[:, j:j + 1] for j in range(10)]
+    FG, FG96 = T.fx[:, NC:2 * NC], T.fx[:, NC:NC + 96]
+    b6, b7 = 6 * 512, 7 * 512
+    TH, CI, CG = ps[:, b6:b6 + 256], ps[:, b6 + 256:b6 + 256 + NC], ps[:, b6 + 384:b6 + 480]
+    FS, AP, LP = ps[:, b7:b7 + 96], ps[:, b7 + 128:b7 + 142], ps[:, b7 + 160:b7 + 176]
+    DE, KEY = ps[:, 0:256], ps[:, 512:768]
+    ZA, ZB, ZW = ps[:, 2304:2560], ps[:, 2560:2576], ps[:, 2304:2576]
+
     dma("s", T.sni[:], T.snd[:], [], ["sni"])
-    dma("y", T.labi[:, PAD:TW], T.lab[:], [], ["labi"])
-    dma("y", T.ldw[:, PAD:TW], T.ld[:], [], ["ldw"])
-    dma("y", W[0][:, PAD + 3072:PAD + 3088], T.rt[:], [], ["w0rt"])
-    dma("y", T.nbw[:, PAD:TW], T.nb[:], [], ["nbw"])
-    dma("y", T.ndw[:, PAD:TW], T.nd[:], [], ["ndw"])
+    dma("y", W[0][:, 0:V], T.d0[:], [], ["w0own"])
+    dma("s", T.fli[0:8, :], T.fl[:], [], ["fli"])
+    dmas("y", [(T.labi[a:a + 15, 0:V], T.lab[a:a + 15, :]) for a in range(0, 128, 16)], [], ["labi"])
+    dma("y", T.ldw[:, 0:V], T.ld[:], [], ["ldw"])
+    dma("y", W[0][:, 3072:3088], T.rt[:], [], ["w0rt"])
     for t in range(RO):
         arrival("aw%d" % t, 3 * ne, ["w%dg" % t])
     for t in range(RO - 1):
-        arrival("af%d" % t, 2 * ne, ["fr%d" % t])
-    arrival("alst", ne, ["lst"])
+        for h in range(2):
+            arrival("af%d%d" % (t, h), ne, ["fr%d%d" % (t, h)])
+    arrival("alst", ne, ["sr"])
 
     iota(T.pidx[:], [[0, 1]], 0, 1, ["pidx"], False)
-    iota(T.va[:], [[-16, 8], [0, 16]], 0, 1, ["va"])
-    iota(T.vb[:], [[1, 128]], 0, -1, ["vb"])
-    iota(T.dumc[:], [[0, 2], [1, 48]], 1600, 0, ["dumc"])
+    iota(T.vc[:], [[1, 144]], -16, -1, ["vc"])
     iota(T.ci[:], [[1, 16]], 0, 0, ["ci"])
-    iota(T.cv[:, 0:272], [[1, 272]], 0, 0, ["cv"])
-    iota(T.vals[:, 0:768], [[1, 48], [96, 16]], PAD, 0, ["valsv"])
-    iota(T.vals[:, 768:V], [[1, 48], [96, 16]], PAD + 48, 0, ["valss"])
+    iota(T.gx[:], [[1, 8], [0, 16]], 0, 0, ["gx"])
+    iota(T.vd[0:32, :], [[1, 144]], -16, -16, ["vd"])
+    send([(peer(1), 0, q4, T.sni[:, 0:32], T.sr[:, 0:32]), (peer(2), q4, 2 * q4, T.sni[:, 32:64], T.sr[:, 32:64]),
+          (peer(3), 2 * q4, ne, T.sni[:, 64:96], T.sr[:, 64:96])], "alst", ["sni"])
+    iota(T.crow[:], [[1, NC]], 0, 0, ["crow"])
+    iota(T.vi[:], [[1, NC]], 0, NC, ["vi"], False)
+    fill(T.hw[:, 0:CAP], CAP, 0, ["hw"])
+    vb = T.vc[:, 16:144]
 
-    ms(T.mx[:], 0.0, ["mx"])
-    ac(T.cs[:, 0:272], T.mx[:], F.Silu, ["mx"], ["cs"])
-    ms(W[0][:, 0:PAD], 255.0, ["w0pad"])
-    ms(T.ldw[:, 0:PAD], 255.0, ["ldpad"])
-    ms(T.ndw[:, 0:PAD], 255.0, ["ndpad"])
+    ms(T.k0[:], -1000.0, ["k0"])
+    ms(T.ones[:], 1.0, ["ones"])
+    ms(T.kt[:], 0.0, ["kt"])
+    ac(T.y1[:], T.kt[:], F.Silu, ["kt"], ["y1"])
     ts(T.pmi[:], T.pidx[:], 15, None, A.bitwise_and, None, ["pidx"], ["pmi"])
     ts(T.gmi[:], T.pidx[:], 16, None, A.bitwise_and, None, ["pidx"], ["gmi"])
-    ts(T.ta[:], T.va[:], 0.0, None, A.is_ge, None, ["va"], ["ta"])
+    ts(T.ggi[:], T.pidx[:], 4, None, A.arith_shift_right, None, ["pidx"], ["ggi"])
+    ms(T.fx[:], 1.0, ["cum", "fg"])
     cp(PM, T.pmi[:], ["pmi"], ["pm"])
-    ts(C48, T.pmi[:], 48.0, None, A.mult, None, ["pmi"], ["c48"])
-    ts(GAM, T.gmi[:], -1.0, None, A.add, None, ["gmi"], ["gam"])
-    ts(T.tb[:], T.vb[:], 0.0, None, A.is_gt, None, ["vb"], ["tb"])
-    ts(T.tc[:], T.va[:], 15.0, None, A.is_le, None, ["va"], ["tc"])
-    tt(T.lt[:], T.ta[:], T.tb[:], A.mult, ["ta", "tb"], ["lt"])
-    tt(T.blk[:], T.ta[:], T.tc[:], A.mult, ["ta", "tc"], ["blk"])
-    ts(T.dum[:], T.dumc[:], C48, None, A.add, None, ["dumc", "c48"], ["dum"])
+    cp(GM, T.gmi[:], ["gmi"], ["gm"])
+    cp(GP, T.ggi[:], ["ggi"], ["gp"])
+    ms(T.fx[:, 0:1], 0.0, ["cum"])
     ts(T.eq[:], T.ci[:], PM, None, A.is_equal, None, ["ci", "pm"], ["eq"])
-    ts(GB, PM, 32.0, GAM, A.mult, A.add, ["pm", "gam"], ["gb"])
+    ts(mat("blk"), T.gx[:], GP, None, A.is_equal, None, ["gx", "gp"], ["blk"])
+    ts(VOFF, GP, -16.0 * NC, None, A.mult, None, ["gp"], ["voff"])
     tt(T.wt[:, 1:16], T.eq[:, 0:15], T.eq[:, 1:16], A.subtract, ["eq"], ["wt"])
-    ts(T.wt[:, 0:1], T.eq[:, 15:16], 8.0, None, A.mult, None, ["eq"], ["wt0"])
+    ts(T.b8[0:32, :], T.vd[0:32, :], 0.0, None, A.is_equal, None, ["vd"], ["b8"])
     cp(T.snu[:], T.sni[:], ["sni"], ["snu"])
-    NS = 7
-    for j in range(NS):
-        ac(mat(j), T.blk[:], F.Identity, ["blk", "wt", "wt0"], ["mat%d" % j], scale=T.wt[:, j:j + 1])
+    ts(T.ta[:], vb, 0.0, None, A.is_ge, None, ["vc"], ["ta"])
+    ts(T.o1[:], T.vc[:], PM, 0.0, A.add, A.is_equal, ["vc", "pm"], ["o1"])
+    cp(E15, T.eq[:, 15:16], ["eq"], ["e15c"])
+    ts(mat("one"), vb, 0.0, None, A.is_equal, None, ["vc"], ["one"])
+    tt(T.tb[:], T.ta[:], mat("blk"), A.mult, ["ta", "blk"], ["tb"])
+    ts(WL, E15, 17.0, -1.0, A.mult, A.add, ["e15c"], ["wl"])
+    ts(T.vj[:], T.vi[:], VOFF, None, A.add, None, ["vi", "voff"], ["vj"])
+    cp(T.flb[0:8, :], T.fli[0:8, :], ["fli"], ["flb"])
+    mms([(FS, lane(T.b8, l, 8), T.flb[0:8, l:V:16]) for l in range(16)], ["b8", "flb"], ["#7"])
+    ts(T.ya[:, 0:7], T.ci[:, 0:7], 16.0, PM, A.mult, A.add, ["ci", "pm"], ["ya"])
+    ms(T.dua[:], 0.0, ["dua"])
+    cp(mat("tri"), T.tb[:], ["tb"], ["tri"])
+    ts(mat("e15"), vb, 0.0, E15, A.is_equal, A.mult, ["vc", "e15c"], ["e15"])
+    ts(T.dua[:, 7:14], T.ya[:, 0:7], -1.0 / 256.0, -0.5, A.mult, A.add, ["ya"], ["dua"])
+    ms(T.mat[:, 128 * MATS.index("tri") + 15:128 * MATS.index("tri") + 128:16], 0.0, ["tri"])
+    ts(DEC, E15, -1.0, None, A.add, None, ["e15c"], ["decc"])
+    fill(T.labi[:, V:TW], CAP, NP - 1, ["labpad"], False)
+    dma("y", T.labi[15:128:16, :], T.vj[:], ["vj", "labpad"], ["lab15", "labpad"])
 
-    def late_constants():
-        ts(T.gl[:], T.ci[:], GB, 1.0, A.add, A.add, ["ci", "gb"], ["gl"])
-        ms(T.labi[:, 0:PAD], NP - 1, ["labpad"])
-        ms(T.nbw[:, 0:PAD], NP - 1, ["nbpad"])
-        ms(W[0][:, PAD + 3088:WW], 255.0, ["w0none"])
-        for j in range(NS, 16):
-            ts(mat(j), T.blk[:], T.wt[:, j:j + 1], None, A.mult, None, ["blk", "wt"], ["mat%d" % j])
-        for j in range(16, 21):
-            ts(mat(j), T.blk[:], T.eq[:, j - 5:j - 4], None, A.mult, None, ["blk", "eq"], ["mat%d" % j])
-        ts(mat(21), T.blk[:], -4096.0, None, A.mult, None, ["blk"], ["mat21"])
+    def pick_d(src, d):
+        a = GS * (d - 1)
+        ac(T.sbf[:, a:a + GS], W[src][:, 0:V].indirect(T.snu[:, 32 * (d - 1):32 * d]), F.Identity,
+           ["w%down" % src, "snu"], ["sbf%d" % d])
 
-    def slot_lists():
-        ts(T.sa[:], T.sni[:], -47.5, 1.0 / 96.0, A.add, A.mult, ["sni"], ["sa"])
-        ts(KC, PM, -8.0, None, A.add, None, ["pm"], ["kc"])
-        cp(T.sb[:], T.sa[:], ["sa"], ["sb"])
-        ms(T.r2[:], 3328.0, ["r2"])
-        ts(T.sc[:], T.sb[:], 96.0, None, A.mult, None, ["sb"], ["sc"])
-        ms(T.k0[:], 0.0, ["k0"])
-        tt(T.sd[:], T.sc[:], T.sni[:], A.add, ["sc", "sni"], ["sd"])
-        ms(T.y1[:], 0.0, ["y1"])
-        cp(T.su[:, 0:96], T.sd[:], ["sd"], ["su0"])
-        ts(T.su[:, 96:192], T.sd[:], 96.0, None, A.add, None, ["sd"], ["su1"])
-        q = ne // 4
-        send([(peer(1), 0, q, [T.su[:, 0:32]], T.lst[:, 0:32]), (peer(2), q, 2 * q, [T.su[:, 128:160]], T.lst[:, 32:64]),
-              (peer(3), 2 * q, 3 * q, [T.su[:, 64:96]], T.lst[:, 64:96]),
-              (peer(3), 3 * q, 4 * q, [T.su[:, 160:192]], T.lst[:, 96:128])], "alst", ["su0", "su1"])
-        ms(T.y2[:], 0.0, ["y2"])
-        ms(T.k0[:, 0:256:16], 20000.0, ["k0"])
+    def send_d(dstw, d):
+        a = GS * (d - 1)
+        send([(peer(d), 0, ne, T.sbf[:, a:a + GS], W[dstw][:, V + a:V + a + GS])], "aw%d" % dstw, ["sbf%d" % d])
 
-    def send_d(src, dstw):
-        for d in range(1, N):
-            a = GS * (d - 1)
-            ac(T.sbf[:, a:a + GS], W[src][:, PAD:TW].indirect(T.snu[:, 32 * (d - 1):32 * d]), F.Identity,
-               ["w%down" % src, "snu"], ["sbf%d" % d])
-            send([(peer(d), 0, ne, [T.sbf[:, a:a + GS]], W[dstw][:, TW + a:TW + a + GS])], "aw%d" % dstw, ["sbf%d" % d])
-
-    send_d(0, 0)
-    iota(T.gs[:, V:2 * V], [[0, V]], 0, 0, ["gs"])
-    dma("y", T.gv[0:128:16, 0:V], T.gs[0:128:16, V:2 * V], ["gs"], ["gvown"])
+    for d in range(1, N):
+        pick_d(0, d)
+        send_d(0, d)
+    dma("y", T.nbw[:, 0:V], T.nb[:], ["sbf3"], ["nbw"])
+    dma("y", T.ndw[:, 0:V], T.nd[:], [], ["ndw"])
+    fill(T.nbw[:, V:TW], CAP, NP - 1, ["nbpad"], False)
+    fill(T.gs[:, V:2 * V], V, 0, ["gs"])
+    dma("y", T.gv[:, 0:V], T.gs[:, V:2 * V], ["gs"], ["gvown"])
+    dma("y", T.gs[:, 0:V], T.gs[:, V:2 * V], ["gs"], ["gsown"])
+    dma("y", T.gv[:, V:2 * V], T.gs[:, V:2 * V], ["gs"], ["gv"])
     dma("y", T.ov[0:128:16, :], T.gs[0:128:8, V:2 * V], ["gs"], ["ov"])
     dma("y", T.ow[0:128:16, :], T.gs[0:128:8, V:2 * V], ["gs"], ["ow"])
-    dma("y", T.gs[0:128:16, 0:V], T.gs[0:128:16, V:2 * V], ["gs"], ["gsown"])
+
+    for i in range(1, 16):
+        ac(mat("d%d" % i), mat("blk"), F.Identity, ["blk", "wt"], ["d%d" % i], scale=T.wt[:, i:i + 1])
+    ac(mat("l14"), mat("blk"), F.Identity, ["blk", "eq"], ["l14"], scale=T.eq[:, 14:15])
+    DM = ["d%d" % i for i in range(1, 16)] + ["l14", "p512", "ones"]
+
+    def late_constants(step):
+        if step == 0:
+            ts(T.ta[:], vb, 0.0, 4095.0, A.is_equal, A.mult, ["vc"], ["ta"])
+            ts(T.dec[:], T.ones[:], DEC, None, A.mult, None, ["ones", "decc"], ["dec"])
+            ts(MINS, E15, 999.0, 1.0, A.mult, A.add, ["e15c"], ["mins"])
+            tt(mat("trs"), T.tb[:], T.ta[:], A.add, ["ta", "tb"], ["trs"])
+            ts(T.o2[:], T.o1[:], WL, None, A.mult, None, ["o1", "wl"], ["o2"])
+        if step == 1:
+            ms(T.ldw[:, V:TW], 255.0, ["ldpad"])
+            ts(mat("p512"), vb, 0.0, 512.0, A.is_equal, A.mult, ["vc"], ["p512"])
+            ts(KD, PM, -8.0, 1.0 / 32.0, A.add, A.mult, ["pm"], ["kdc"])
+            ts(GB, PM, 32.0, GM, A.mult, A.add, ["pm", "gm"], ["gb"])
+            ts(mat("l15"), mat("blk"), E15, None, A.mult, None, ["blk", "e15c"], ["l15"])
+            ts(mat("n15"), mat("blk"), E15, -1.0, A.mult, A.mult, ["blk", "e15c"], ["n15"])
+        if step == 2:
+            ms(W[0][:, 3088:WW], 255.0, ["w0none"])
+            ms(T.ndw[:, V:TW], 255.0, ["ndpad"])
+            ts(mat("neg"), vb, 0.0, -1.0, A.is_equal, A.mult, ["vc"], ["neg"])
+            ts(mat("n512"), vb, 0.0, -512.0, A.is_equal, A.mult, ["vc"], ["n512"])
+            ts(mat("kd"), vb, 0.0, KD, A.is_equal, A.mult, ["vc", "kdc"], ["kd"])
+            ts(mat("sum4k"), mat("blk"), -4096.0, None, A.mult, None, ["blk"], ["sum4k"])
+            ts(T.gl[:], T.ci[:], GB, None, A.add, None, ["ci", "gb"], ["gl"])
+            ts(T.idf[:], vb, 0.0, None, A.is_equal, None, ["vc"], ["idf"])
+            ts(T.b3[:], T.vc[:], 0.0, -1.0, A.is_equal, A.mult, ["vc"], ["b3"])
+            ts(T.sa[:], T.sr[:], 15, None, A.bitwise_and, None, ["sr"], ["sa"])
+            ts(T.sb[:], T.sr[:], 4, None, A.arith_shift_right, None, ["sr"], ["sb"])
+            ts(T.b2[:], T.b3[:], T.eq[:, 0:1], None, A.mult, None, ["b3", "eq"], ["b2"])
+            ts(T.sc[:], T.sa[:], 96.0, None, A.mult, None, ["sa"], ["sc"])
+            ms(T.k0[:, 0:256:16], -256.75, ["k0"])
+            ms(T.y2[:], 0.0, ["y2"])
+            tt(T.sd[:], T.sc[:], T.sb[:], A.add, ["sc", "sb"], ["sd"])
+            ms(T.r2[:], 3328.0, ["r2"])
+            cp(T.lst[:], T.sd[:], ["sd"], ["lst"])
 
     for t in range(RO):
         last = t == RO - 1
         c = 12 + t
         wn = "w%d" % t
-        wown = [wn + "own", wn + "pad"]
         wall = [wn + "own", wn + "g", wn + "rt", wn + "none"]
-        if t == 0:
-            raw, rn, th = T.fli[:], "fli", 0.5
-        else:
+        if t > 0:
             R = T["fr%d" % (t - 1)]
-            tt(T.x2[:], R[:, 0:192], R[:, 192:384], A.max, ["fr%d" % (t - 1), "oc%d" % (t - 1)], ["x2"])
-            tt(T.raw[:], T.x2[:, 0:96], T.x2[:, 96:192], A.max, ["x2"], ["raw"])
-            raw, rn, th = T.raw[:], "raw", 100.0 * t - 50.0
-        ts(T.fg[:], raw, th, None, A.is_ge, None, [rn], ["fg"])
-        ts(T.fb[:], raw, th, 8192.0, A.is_ge, A.mult, [rn], ["fb"])
-        scan(T.pl[:], T.fg[:], T.fg[:], A.add, A.max, ["fg"], ["pl"])
-        ex = ps[:, 7 * 512 + 256:7 * 512 + 257]
-        mms([(ex, T.lt[:], T.pl[:, 95:96], True, True)], ["lt", "pl"], ["b7"])
-        tt(T.yy[:], T.dum[:], T.fb[:], A.subtract, ["dum", "fb"], ["yy"])
-        tt(T.xx[:], T.pl[:], T.yy[:], A.max, ["pl", "yy"], ["xx"])
-        ts(T.off[:], T.xx[:], ex, GAM, A.add, A.add, ["xx", "b7", "gam"], ["off"])
-        cp(T.cv[:].indirect(T.off[:, 0:48]), T.vals[:, 0:768], ["off", "valsv", "cv"], ["cv"])
-        ac(T.cs[:].indirect(T.off[:, 48:96]), T.vals[:, 768:V], F.Silu, ["off", "valss", "cs"], ["cs"])
+            mms([(FS, lane(T.b3, 0), R[:, 96 * j:96 * j + 96], False, j == 1) for j in range(2)], ["b3", "fr%d0" % (t - 1)], ["#7"])
+            tt(T.two[:], R[:, 192:288], R[:, 288:384], A.add, ["fr%d1" % (t - 1)], ["two"])
+            tt(FG96, T.two[:], FS, A.is_ge, ["two", "#7"], ["fg"])
+        else:
+            ts(FG96, FS, 0.5, None, A.is_ge, None, ["#7"], ["fg"])
+        scan(T.fx[:, 1:NC], T.fx[:, NC:2 * NC - 1], T.fx[:, NC:2 * NC - 1], A.add, A.max, ["fg"], ["cum"])
+        mms([(CI, mat("tri"), FG), (CI, mat("e15"), T.crow[:])], ["tri", "e15", "fg", "crow"], ["#6"])
+        mms([(AP, mat("one"), T.dua[:, 0:14])] + [(AP, lane(T.o1, l), T.fx[:, l:2 * NC:16]) for l in range(16)],
+            ["one", "dua", "o1", "cum", "fg"], ["#7"])
+        ac(T.cis[:], CI, F.Identity, ["#6"], ["cis"])
         if t == 0:
-            late_constants()
-        tt(T.mx[:], T.cv[:, 0:272], T.cs[:, 0:272], A.max, ["cv", "cs"], ["mx"])
-        tr32(T.tt[:, 0:256], T.mx[:, 0:256], ["mx"], ["tt0"])
-        tr32(T.tt[:, 256:512], T.mx[:, 16:272], ["mx"], ["tt1"])
-        ts(T.tl[:], T.tt[:].indirect(T.gl[:, 0:2]), 0.25, None, A.add, None, ["tt0", "tt1", "gl"], ["tl"])
-        L = T.tl[:, 0:16]
+            late_constants(0)
+        elif not last:
+            ms(T.y2[:, c - 1:256:16], 0.0, ["y2"])
+        if not last:
+            mms([(CG, mat("blk"), T.fx[:, 0:96]), (CG, mat("trs"), FG96)], ["blk", "trs", "cum", "fg"], ["#6"])
+        ts(T.yb[:, 0:7], ps[:, b7 + 135:b7 + 142], -4096.0, None, A.mult, None, ["#7"], ["yb"])
+        tt(T.yc[:, 0:7], ps[:, b7 + 128:b7 + 135], T.yb[:, 0:7], A.max, ["#7", "yb"], ["yc"])
+        cp(T.off[:, 0:7], T.yc[:, 0:7], ["yc"], ["off"])
+        cp(T.hw[:].indirect(T.off[:, 0:7]), T.cis[:], ["off", "cis"], ["hw"])
+        scan(T.hg[:], T.dec[:], T.hw[:, 0:CAP], A.add, A.max, ["dec", "hw"], ["hg"])
+        ts(T.hm[:], T.hg[:], MINS, None, A.min, None, ["hg", "mins"], ["hm"])
+        mms([(LP, lane(T.o2, l), T.hm[:, l:CAP:16]) for l in range(16)], ["o2", "hm"], ["#7"])
+        if not last:
+            fill(T.hw[:, 0:CAP], CAP, 0, ["hw"])
+            ts(T.rem[:], CG, 4096.0 + CAP - 0.5, 0.9 * STAMP[t], A.is_lt, A.mult, ["#6"], ["rem"])
+        if t == 0:
+            late_constants(1)
+        elif not last:
+            ms(T.y1[:, c - 1:256:16], 0.0, ["y1"])
+        ts(T.tl[:], LP, 15.0, None, A.add, None, ["#7"], ["tl"])
+        L = T.tl[:]
         ac(T.ldt[:], T.ldw[:].indirect(L), F.Identity, ["ldw", "ldpad", "tl"], ["ldt"])
         if t == 0:
             cp(T.labu[:], T.labi[:].indirect(L), ["labi", "labpad", "tl"], ["labu"])
-            slot_lists()
-        else:
-            cp(T.labu[:], T.labf[:].indirect(L), ["labf", "tl"], ["labu"])
-        if not last:
-            iota(T.cv[:, 0:272], [[1, 272]], 0, 0, ["cv"])
-            iota(T.cs[:, 0:272], [[0, 272]], 0, 0, ["cs"])
-        if t == 0:
+            late_constants(2)
             iota(T.r1[:], [[1, 272]], -224, 0, ["r1"])
-            iota(T.st[:], [[100, 3], [0, 256]], 100, 0, ["st"])
-            iota(T.gv[:, V:2 * V], [[0, V]], 0, 0, ["gv"])
+            for j in range(RO - 1):
+                fill(T.st[:, 256 * j:256 * j + 256], 256, STAMP[j], ["st%d" % j])
             comp("g", lambda: g.affine_select(T.labf[:], T.labi[:], [[0, TW]], A.is_ge, 0.0, 1, 0),
                  ["labi", "labpad"], ["labf"])
-        win = W[t][:, PAD:PAD + NP]
+        else:
+            cp(T.labu[:], T.labf[:].indirect(L), ["labf", "tl"], ["labu"])
+        if t == 1:
+            fill(T.lo[:], TW, NP - 1, ["lo"])
+        win = W[t][:, 0:NP]
 
-        def gather(q, u0, u1):
-            lu, nm = (T.labu, "labu") if u0 < 8 else (T.nbu, "nbu")
-            o = lu[:, 32 * (u0 % 8):32 * (u0 % 8) + 32 * (u1 - u0)]
-            out = T.gt[:, 512 * u0:512 * u1]
-            wr = ["gt%d" % u for u in range(u0, u1)]
+        def gather(q, h0, h1):
+            lu, nm = (T.labu, "labu") if h0 < 16 else (T.nbu, "nbu")
+            o = lu[:, 16 * (h0 % 16):16 * (h0 % 16 + h1 - h0)]
+            out = T.gt[:, 256 * h0:256 * h1]
+            wr = ["gt%d" % h for h in range(h0, h1)]
             if q == "v":
                 cp(out, win.indirect(o), wall + [nm], wr)
             else:
@@ -302,163 +368,137 @@ def rank_program(g, core, T, topo):
 
         def diffs(u):
             b = u % 6
-            a = 32 * (u % 8)
-            lst = [(ps[:, 512 * b:512 * b + 512:16], mat(0), T.ldt[:, a:a + 32], True, True)]
+            src = (T.ldt if u < 8 else T.ndt)[:, 32 * (u % 8):32 * (u % 8) + 32]
+            lst = [(ps[:, 512 * b:512 * b + 512:16], mat("p512"), T.ones[:, 0:32], True, True)] if u < 6 else []
             for i in range(1, 16):
-                out = ps[:, 512 * b + i:512 * b + 512:16]
-                if u >= 8:
-                    lst.append((out, mat(i), T.ndt[:, a:a + 32], True, True))
-                elif i == c:
-                    lst.append((out, mat(16 + c - 12), T.ldt[:, a:a + 32], True, True))
-                elif i < c or b >= 4 or (t == 0 and u < 6):
-                    lst.append((out, mat(i), T.ldt[:, a:a + 32], True, True))
-            mms(lst, ALLM + ["ldt"] + (["ndt"] if u >= 8 else []), ["b%d" % b])
+                lst.append((ps[:, 512 * b + i:512 * b + 512:16], mat("l14" if u < 8 and i == 15 else "d%d" % i), src, True, True))
+            mms(lst, DM + ["ldt" if u < 8 else "ndt"], ["#%d" % b])
 
-        def least(u0, u1):
-            b = u0 % 6
-            scan(T.sn[:, 512 * u0:512 * u1], ps[:, 512 * b:512 * (b + u1 - u0)], T.gt[:, 512 * u0:512 * u1], A.add, A.min,
-                 ["b%d" % (u % 6) for u in range(u0, u1)] + ["gt%d" % u for u in range(u0, u1)],
-                 ["sn%d" % u for u in range(u0, u1)])
+        def least(h0, h1):
+            b = h0 % 12
+            scan(T.sn[:, 256 * h0:256 * h1], ps[:, 256 * b:256 * (b + h1 - h0)], T.gt[:, 256 * h0:256 * h1], A.add, A.min,
+                 sorted(set("#%d" % (h // 2 % 6) for h in range(h0, h1))) + ["gt%d" % h for h in range(h0, h1)],
+                 ["sn%d" % h for h in range(h0, h1)])
 
+        gtl = ["gt%d" % h for h in range(16)]
+        snl, snn = ["sn%d" % h for h in range(16)], ["sn%d" % h for h in range(16, 32)]
+        old, thr, sc = T.gt[:, 15:4096:16], T.sn[:, 15:4096:16], T.sn[:, 4096 + 15:8192:16]
         for u in range(6):
             diffs(u)
-        gather("s", 2, 4)
-        gather("v", 0, 2)
-        cp(T.nbu[:], T.nbw[:].indirect(L), ["nbw", "nbpad", "tl"], ["nbu"])
+        gather("s", 4, 8)
+        gather("v", 0, 4)
+        gather("s", 8, 12)
         ac(T.ndt[:], T.ndw[:].indirect(L), F.Identity, ["ndw", "ndpad", "tl"], ["ndt"])
-        gather("s", 4, 6)
-        gather("s", 6, 8)
-        least(0, 2)
+        gather("s", 12, 16)
+        least(0, 4)
         diffs(6)
         diffs(7)
-        least(2, 4)
-        n15 = ps[:, 6 * 512:6 * 512 + 256]
-        mms([(n15, mat(20), T.ndt[:], True, True)], ["mat20", "ndt"], ["b6"])
+        least(4, 8)
+        cp(T.nbu[:], T.nbw[:].indirect(L), ["nbw", "nbpad", "tl"], ["nbu"])
         diffs(8)
         diffs(9)
-        cp(T.old[:], W[t][:, 0:TW].indirect(L), wown + ["tl"], ["old"])
-        least(4, 6)
+        if XV:
+            gather("v", 16, 16 + XV)
+        least(8, 12)
         diffs(10)
         diffs(11)
-        gather("s", 8, 10)
-        gather("s", 10, 12)
-        gather("s", 12, 14)
-        gather("s", 14, 15)
-        gather("s", 15, 16)
+        for a, b in zip((16 + XV,) + CUTS, CUTS + (32,)):
+            gather("s", a, b)
         if not last:
-            ac(T.nb32[:], T.nbw[:].indirect(T.tl[:, 0:17]), F.Identity, ["nbw", "nbpad", "tl"], ["nb32"])
-        ac(T.lab32[:], T.labf[:].indirect(L), F.Identity, ["labf", "tl"], ["lab32"])
-        least(6, 8)
+            ac(T.nb32[:, 0:256], T.nbw[:].indirect(L), F.Identity, ["nbw", "nbpad", "tl"], ["nb32"])
+            ac(T.lab32[:], T.labf[:].indirect(L), F.Identity, ["labf", "tl"], ["lab32"])
+            ac(T.nb32[:, 256:272], T.nb32[:, 0:16], F.Identity, ["nb32"], ["nb32b"])
+        least(12, 16)
         diffs(12)
         diffs(13)
-        th2 = ps[:, 7 * 512:7 * 512 + 256]
-        tt(T.thr[:], T.sn[:, c:4096:16], T.old[:], A.min, ["sn%d" % u for u in range(8)] + ["old"], ["thr"])
-        least(8, 10)
+        mms([(TH, mat("one"), thr), (TH, mat("n15"), T.ndt[:])], ["one", "n15", "ndt"] + snl, ["#6"])
+        least(16, 20)
         diffs(14)
         diffs(15)
-        tt(th2, T.thr[:], n15, A.subtract, ["thr", "b6"], ["b7"])
-        if last:
-            ms(T.y1[:, c - 1:256:16], 0.0, ["y1"])
-        least(10, 12)
-        za, zb, zw = ps[:, 2304:2560], ps[:, 2560:2576], ps[:, 2304:2576]
+        least(20, 24)
         if not last:
-            mms([(za, mat(20), T.r2[:, 0:256], True, False), (za, mat(20), T.r1[:, 0:256], False, False),
-                 (zb, mat(20), T.r2[:, 256:272], True, False), (zb, mat(20), T.r1[:, 256:272], False, False)],
-                ["mat20", "r1", "r2"], ["b4", "b5"])
-        least(12, 14)
-        least(14, 15)
-        least(15, 16)
-        sc = T.sn[:, 4096 + 15:8192:16]
-        scn = ["sn%d" % u for u in range(8, 16)]
-        tt(T.up[:], sc, th2, A.is_lt, scn + ["b7"], ["up"])
-        ac(T.nu[:], T.up[:], F.Identity, ["up"], ["nu"], scale=-512.0, bias=512.0)
-        tt(T.cand[:], sc, n15, A.add, scn + ["b6"], ["cand"])
+            mms([(ZA, mat("one"), T.r2[:, 0:256], True, False), (ZA, mat("one"), T.r1[:, 0:256], False, False),
+                 (ZB, mat("one"), T.r2[:, 256:272], True, False), (ZB, mat("one"), T.r1[:, 256:272], False, False)],
+                ["one", "r1", "r2"], ["#4", "#5"])
+        least(24, 28)
+        mms([(DE, mat("l15"), T.ndt[:], True, False), (DE, mat("neg"), old, False, False),
+             (KEY, mat("l15"), T.ndt[:], True, False), (KEY, mat("kd"), T.ones[:], False, False)],
+            ["l15", "neg", "kd", "ndt", "ones"] + gtl, ["#0", "#1"])
+        for a, b in zip((28,) + LAST, LAST + (32,)):
+            least(a, b)
+        tt(T.up[:], sc, TH, A.is_lt, snn + ["#6"], ["up"])
+        mms([(DE, mat("one"), sc, False, True), (KEY, mat("one"), sc, False, False)], ["one"] + snn, ["#0", "#1"])
+        if not last:
+            mms([(ZA, mat("sum4k"), T.up[:], False, True), (ZB, mat("sum4k"), T.up[:, 0:16], False, True)],
+                ["sum4k", "up"], ["#4", "#5"])
+        mms([(KEY, mat("n512"), T.up[:], False, True)], ["n512", "up"], ["#1"])
+        tt(T.dm[:], T.up[:], DE, A.mult, ["up", "#0"], ["dm"])
 
-        def new_d(step):
-            if step == 0:
-                tt(T.cm[:], T.cand[:], T.nu[:], A.max, ["cand", "nu"], ["cm"])
-            if step == 1:
-                tt(T.dnew[:], T.cm[:], T.old[:], A.min, ["cm", "old"], ["dnew"])
-            if step == 2:
-                cp(W[t][:, 0:TW].indirect(L), T.dnew[:], ["dnew", "tl"], wown)
+        def new_d():
+            tt(W[t][:, 0:TW].indirect(L), old, T.dm[:], A.add, gtl + ["dm", "tl"], [wn + "own", wn + "g"])
 
-        def new_labels(fill):
-            if last:
-                ac(T.key[:], T.cm[:], F.Identity, ["cm", "kc"], ["key"], scale=32.0, bias=KC)
-            else:
-                ts(T.key[:], T.cm[:], 32.0, KC, A.mult, A.add, ["cm", "kc"], ["key"])
-            fill(0)
-            tr32(T.kt[:], T.key[:], ["key"], ["kt"])
-            fill(1)
-            scan(T.ks[:], T.k0[:], T.kt[:], A.add, A.min, ["k0", "kt"], ["ks"])
-            fill(2)
-            ts(T.q1[:], T.ks[:, 15:256:16], 8168.0, 1.0 / 32.0, A.min, A.mult, ["ks"], ["q1"])
-            if t > 0 and not last:
-                ms(T.y1[:, c - 1:256:16], 0.0, ["y1"])
-            cp(T.li[:], T.q1[:], ["q1"], ["li"])
-            if t > 0 and not last:
-                ms(T.y2[:, c - 1:256:16], 0.0, ["y2"])
-            tt(T.df[:], T.q1[:], T.li[:], A.subtract, ["q1", "li"], ["df"])
-            if not last:
-                ts(T.y2[:, c:256:16], T.li[:], -255.0, None, A.add, None, ["li"], ["y2"])
-            ts(T.y1[:, c:256:16], T.df[:], 32.0, -8.0, A.mult, A.add, ["df"], ["y1"])
-            if not last:
-                tr32(T.d2[:], T.y2[:], ["y2"], ["d2"])
-            tr32(T.d1[:], T.y1[:], ["y1"], ["d1"])
-            if not last:
-                tt(T.ldw[:].indirect(L), T.ldt[:], T.d2[:], A.add, ["ldt", "d2", "tl"], ["ldw", "ldpad"])
-            tt(T.labf[:].indirect(L), T.lab32[:], T.d1[:], A.add, ["lab32", "d1", "tl"], ["labf"])
+        def least_key():
+            scan(T.ks[:], T.k0[:], T.kt[:], A.max, A.min, ["k0", "kt"], ["ks"], -1000.0)
+            ts(T.y2[:, c:256:16], T.ks[:, 15:256:16], ROUND, 257.0 - ROUND, A.add, A.add, ["ks"], ["y2"])
 
         if last:
-            def tail(step):
-                if step == 0:
-                    new_d(1)
-                    new_d(2)
-                    dma("y", T.yd[:], W[t][:, PAD:TW], [wn + "own"], ["yd"])
-            new_d(0)
-            new_labels(tail)
-            dma("y", T.yl[15:128:16, :], T.labf[15:128:16, PAD:TW], ["labf"], ["yl"])
+            tr32(T.kt[:], KEY, ["#1"], ["kt"])
+            new_d()
+            dma("y", T.yd[:], W[t][:, 0:V], [wn + "own"], ["yd"])
+            least_key()
+            tt(T.y1[:, c:256:16], T.ks[:, 15:256:16], T.y2[:, c:256:16], A.subtract, ["ks", "y2"], ["y1"])
+            tr32(T.d1[:], T.y1[:], ["y1"], ["d1"])
+            ts(T.lo[:].indirect(L), T.d1[:], 32.0, NP - 1.0 + 257.0 * 32.0 - 8.0, A.mult, A.add, ["d1", "tl"], ["lo"])
+            dma("s", T.yl[15:128:16, :], T.lo[15:128:16, 0:V], ["lo"], ["yl"])
             break
-        mms([(za, mat(21), T.up[:], False, True), (zb, mat(21), T.up[:, 0:16], False, True)], ["mat21", "up"], ["b4", "b5"])
-        tt(T.zz[:], T.nb32[:], zw, A.max, ["nb32", "b4", "b5"], ["zz"])
+        tt(T.zz[:], T.nb32[:], ZW, A.max, ["nb32", "nb32b", "#4", "#5"], ["zz"])
         tr32(T.tt[:, 0:256], T.zz[:, 0:256], ["zz"], ["tt0"])
         tr32(T.tt[:, 256:512], T.zz[:, 16:272], ["zz"], ["tt1"])
-        cp(T.xo[:, 0:160], T.tt[:].indirect(T.gl[:, 0:10]), ["tt0", "tt1", "gl"], ["xo0"])
-        cp(T.xo[:, 160:256], T.tt[:].indirect(T.gl[:, 10:16]), ["tt0", "tt1", "gl"], ["xo1"])
+        cp(T.xo[:, 0:128], T.tt[:].indirect(T.gl[:, 0:8]), ["tt0", "tt1", "gl"], ["xo0"])
+        cp(T.xo[:, 128:256], T.tt[:].indirect(T.gl[:, 8:16]), ["tt0", "tt1", "gl"], ["xo1"])
         stamp = T.st[:, 256 * t:256 * (t + 1)]
-        for i in range(9):
-            ac(T.gs[:].indirect(T.xo[:, 16 * i:16 * i + 16]), stamp, F.Silu, ["xo0", "st"], ["gs", "gsown"])
-        for i in range(9, 16):
-            cp(T.gv[:].indirect(T.xo[:, 16 * i:16 * i + 16]), stamp, ["xo0" if i < 10 else "xo1", "st"], ["gv", "gvown"])
-            new_d(i - 9)
-        dma("y", W[t + 1][:, 0:TW], W[t][:, 0:TW], wown, ["w%down" % (t + 1), "w%dpad" % (t + 1)])
-        dma("y", T.ev[:], T.gv[0:128:16, 0:V], ["gv"], ["ev"])
-        dma("y", T.es[:], T.gs[0:128:16, 0:V], ["gs"], ["es"])
-        tt(T.ov[:].indirect(T.lst[:, 0:64]), T.gv[:, V:V + 2 * GS], T.gs[:, V:V + 2 * GS], A.max, ["lst", "gv", "gs"], ["ov"])
-        ac(T.ow[:].indirect(T.lst[:, 64:96]), T.gs[:, V + 2 * GS:2 * V], F.Silu, ["lst", "gs"], ["ow"])
-        ac(T.ow[:].indirect(T.lst[:, 96:128]), T.gv[:, V + 2 * GS:2 * V], F.Silu, ["lst", "gv"], ["ow"])
-        dma("y", T.xv[:], T.ov[0:128:16, :], ["ov"], ["xv"])
-        dma("s", T.xs[:], T.ow[0:128:16, :], ["ow"], ["xs"])
+        new_d()
+        for i in range(8, 16):
+            cp(T.gv[:].indirect(T.xo[:, 16 * i:16 * i + 16]), stamp, ["xo1", "st%d" % t], ["gv", "gvown"])
+        for i in range(8):
+            ac(T.gs[:].indirect(T.xo[:, 16 * i:16 * i + 16]), stamp, F.Silu, ["xo0", "st%d" % t], ["gs", "gsown"])
+            if i == 2:
+                pick_d(t, 1)
+                send_d(t + 1, 1)
+            if i == 4:
+                ac(W[t + 1][:, 3072:WW], W[0][:, 3072:WW], F.Identity, ["w0rt", "w0none"],
+                   ["w%drt" % (t + 1), "w%dnone" % (t + 1)])
+        dma("y", W[t + 1][:, 0:V], W[t][:, 0:V], [wn + "own"], ["w%down" % (t + 1)])
         R = T["fr%d" % t]
-        h = ne // 2
-        send([(peer(-1), 0, h, [T.xv[:, 0:96]], R[:, 0:96]), (peer(-2), h, ne, [T.xv[:, 96:192]], R[:, 96:192])],
-             "af%d" % t, ["xv"])
-        send([(peer(-3), 0, ne, [T.xs[:, 0:96], T.xs[:, 96:192]], R[:, 192:288])], "af%d" % t, ["xs"])
-        send_d(t, t + 1)
-        ac(W[t + 1][:, PAD + 3072:WW], W[0][:, PAD + 3072:WW], F.Identity, ["w0rt", "w0none"],
-           ["w%drt" % (t + 1), "w%dnone" % (t + 1)])
-        ts(T.beyond[:], T.pl[:], ex, 256.0, A.add, A.is_gt, ["pl", "b7"], ["beyond"])
-
-        def own_flags(step):
-            if step == 0:
-                tt(T.rem[:], T.beyond[:], T.fb[:], A.mult, ["beyond", "fb"], ["rem"])
-            if step == 1:
-                tt(T.oc[:], T.ev[:], T.rem[:], A.max, ["ev", "rem"], ["oc"])
-            if step == 2:
-                tt(R[:, 288:384], T.oc[:], T.es[:], A.max, ["oc", "es"], ["oc%d" % t])
-        new_labels(own_flags)
+        for h in range(2):
+            a = V + GS * h
+            tt(T.ov[:, V * h:V * h + V].indirect(T.lst[:, 32 * h:32 * h + 32]), T.gv[:, a:a + GS], T.gs[:, a:a + GS], A.max,
+               ["lst", "gv", "gs", "ov"], ["ov%d" % h])
+            ac(T.ow[:, V * h:V * h + V].indirect(T.lst[:, 64:96]), (T.gs, T.gv)[h][:, V + 2 * GS:2 * V], F.Silu,
+               ["lst", ("gs", "gv")[h], "ow"], ["ow%d" % h])
+            dma("y", T.xf[:, 192 * h + 96:192 * h + 192], T.ow[0:128:16, V * h:V * h + V], ["ow%d" % h], ["xw%d" % h])
+            dma("y", T.xf[:, 192 * h:192 * h + 96], T.ov[0:128:16, V * h:V * h + V], ["ov%d" % h], ["xv%d" % h])
+        for h in range(2):
+            a = 192 * h
+            send([(peer(-1 - h), 0, 2 * q4, T.xf[:, a:a + 96], R[:, a:a + 96]),
+                  (peer(-3), 2 * q4, ne, T.xf[:, a + 96:a + 192], R[:, a + 96:a + 192])], "af%d%d" % (t, h),
+                 ["xv%d" % h, "xw%d" % h])
+        for d in (2, 3):
+            pick_d(t, d)
+            send_d(t + 1, d)
+        mms([(FS, T.idf[:], T.rem[:], True, False)]
+            + [(FS, lane(T.b2, l), T.gs[:, l:V:16], False, False) for l in range(16)], ["idf", "b2", "rem", "gs"], ["#7"])
+        mms([(FS, lane(T.b2, l), T.gv[:, l:V:16], False, False) for l in range(16)], ["b2", "gv"], ["#7"])
+        tr32(T.kt[:], KEY, ["#1"], ["kt"])
+        least_key()
+        tt(T.df[:], T.ks[:, 15:256:16], T.y2[:, c:256:16], A.subtract, ["ks", "y2"], ["df"])
+        tr32(T.d2[:], T.y2[:], ["y2"], ["d2"])
+        ts(T.y1[:, c:256:16], T.df[:], 32.0, 257.0 * 32.0 - 8.0, A.mult, A.add, ["df"], ["y1"])
+        tt(T.ldw[:].indirect(L), T.ldt[:], T.d2[:], A.add, ["ldt", "d2", "tl"], ["ldw", "ldpad"])
+        tr32(T.d1[:], T.y1[:], ["y1"], ["d1"])
+        tt(T.labf[:].indirect(L), T.lab32[:], T.d1[:], A.add, ["lab32", "d1", "tl"], ["labf"])
         if t == RO - 2:
-            dma("y", T.yl[:], T.labf[:, PAD:TW], ["labf", "w%dg" % (t + 1)], ["yl"])
+            dma("y", T.yl[:], T.labf[:, 0:V], ["labf", "w%dg" % (t + 1)], ["yl"])
 
     num = {}
     for o in ops:

@@ -12,18 +12,19 @@ HW = 3840
 GW = 3376
 STAMP = (32.0, 256.0, 2048.0)
 ROUND = 1.5 * 2.0 ** 23
-XV, CUTS, LAST = 1, (20, 24, 28, 30, 31), (30, 31)
+XV = 2
+CUTS, LAST = (20, 24, 28, 30, 31), (30, 31)
 MATS = ["d%d" % i for i in range(1, 16)] + "l14 l15 n15 one neg p512 n512 kd sum4k tri e15 blk trs".split()
 
 SCRATCH = {"ps": ("psum", [128, 4096], "float32")}
 for names, width, kind in (
         ("nbw labi", TW, "int32"), ("labf lo", TW, "float32"), ("ndw ldw", TW, "bfloat16"),
         ("fli", V, "int32"), ("flb sbf", V, "bfloat16"), ("sni sr sa sb sc sd", 96, "int32"), ("snu lst", 96, "uint16"),
-        ("off", 8, "uint16"), ("vi vj", NC, "int32"),
+        ("off", 8, "uint16"), ("vj", NC, "int32"),
         ("rem two", 96, "float32"), ("xf", 384, "float32"), ("fx", 2 * NC, "bfloat16"), ("crow cis", NC, "bfloat16"),
         ("hw", HW, "bfloat16"), ("gv gs", GW, "float32"), ("ov ow", 3072, "float32"),
         ("gt sn", 8192, "bfloat16"), ("mat", len(MATS) * 128, "bfloat16"),
-        ("vc vd b2 b3", 144, "float32"), ("o1 o2 b8", 144, "bfloat16"), ("gx idf ta tb", 128, "float32"),
+        ("vc b2 b3", 144, "float32"), ("o1 o2 b8", 144, "bfloat16"), ("gx idf ta tb", 128, "float32"),
         ("pidx pmi gmi ggi", 1, "int32"), ("col", 16, "float32"), ("ci eq wt df ya yb yc", 16, "float32"),
         ("dua", 16, "bfloat16"), ("gl", 16, "uint16"), ("tl", 16, "uint16"),
         ("r1 r2", 272, "bfloat16"), ("st", 768, "float32"), ("zz nb32", 272, "float32"), ("tt", 512, "float32"),
@@ -143,6 +144,9 @@ def rank_program(g, core, T, topo):
     def ac(out, in_, func, rd, wr, **kw):
         comp("s", lambda: act.activation(out, in_, func, **kw), rd, wr)
 
+    def scaled(out, src, scale, rd, wr):
+        ac(out, src, F.Identity, rd, wr, scale=scale)
+
     def iota(out, pat, base, cm, wr, flt=True):
         if flt:
             comp("g", lambda: g.iota(out, pat, base, cm, allow_small_or_imprecise_dtypes=True), [], wr)
@@ -171,7 +175,7 @@ def rank_program(g, core, T, topo):
     def lane(buf, l, rows=128):
         return buf[0:rows, 16 - l:144 - l]
 
-    PM, GP, GB, KD, E15, WL, MINS, DEC, VOFF, GM = [T.col[:, j:j + 1] for j in range(10)]
+    PM, GP, GB, KD, E15, WL, MINS, DEC, VOFF, GM, PP, P15 = [T.col[:, j:j + 1] for j in range(12)]
     FG, FG96 = T.fx[:, NC:2 * NC], T.fx[:, NC:NC + 96]
     b6, b7 = 6 * 512, 7 * 512
     TH, CI, CG = ps[:, b6:b6 + 256], ps[:, b6 + 256:b6 + 256 + NC], ps[:, b6 + 384:b6 + 480]
@@ -180,13 +184,13 @@ def rank_program(g, core, T, topo):
     ZA, ZB, ZW = ps[:, 2304:2560], ps[:, 2560:2576], ps[:, 2304:2576]
 
     dma("s", T.sni[:], T.snd[:], [], ["sni"])
+    dma("y", T.fli[0:8, :], T.fl[:], [], ["fli"])
     dma("y", W[0][:, 0:V], T.d0[:], [], ["w0own"])
-    dma("s", T.fli[0:8, :], T.fl[:], [], ["fli"])
     dmas("y", [(T.labi[a:a + 15, 0:V], T.lab[a:a + 15, :]) for a in range(0, 128, 16)], [], ["labi"])
+    dma("s", W[0][:, 3072:3088], T.rt[:], [], ["w0rt"])
     dma("y", T.ldw[:, 0:V], T.ld[:], [], ["ldw"])
-    dma("y", W[0][:, 3072:3088], T.rt[:], [], ["w0rt"])
     for t in range(RO):
-        arrival("aw%d" % t, 3 * ne, ["w%dg" % t])
+        arrival("aw%d" % t, 2 * ne, ["w%dg" % t])
     for t in range(RO - 1):
         for h in range(2):
             arrival("af%d%d" % (t, h), ne, ["fr%d%d" % (t, h)])
@@ -196,66 +200,62 @@ def rank_program(g, core, T, topo):
     iota(T.vc[:], [[1, 144]], -16, -1, ["vc"])
     iota(T.ci[:], [[1, 16]], 0, 0, ["ci"])
     iota(T.gx[:], [[1, 8], [0, 16]], 0, 0, ["gx"])
-    iota(T.vd[0:32, :], [[1, 144]], -16, -16, ["vd"])
+    fill(T.labi[:, V:TW], CAP, NP - 1, ["labpad"], False)
     send([(peer(1), 0, q4, T.sni[:, 0:32], T.sr[:, 0:32]), (peer(2), q4, 2 * q4, T.sni[:, 32:64], T.sr[:, 32:64]),
           (peer(3), 2 * q4, ne, T.sni[:, 64:96], T.sr[:, 64:96])], "alst", ["sni"])
-    iota(T.crow[:], [[1, NC]], 0, 0, ["crow"])
-    iota(T.vi[:], [[1, NC]], 0, NC, ["vi"], False)
-    fill(T.hw[:, 0:CAP], CAP, 0, ["hw"])
     vb = T.vc[:, 16:144]
 
-    ms(T.k0[:], -1000.0, ["k0"])
     ms(T.ones[:], 1.0, ["ones"])
-    ms(T.kt[:], 0.0, ["kt"])
-    ac(T.y1[:], T.kt[:], F.Silu, ["kt"], ["y1"])
+    ms(T.fx[:], 1.0, ["cum", "fg"])
+    ac(T.y1[:], T.ones[:], F.Silu, ["ones"], ["y1"], scale=0.0)
     ts(T.pmi[:], T.pidx[:], 15, None, A.bitwise_and, None, ["pidx"], ["pmi"])
     ts(T.gmi[:], T.pidx[:], 16, None, A.bitwise_and, None, ["pidx"], ["gmi"])
     ts(T.ggi[:], T.pidx[:], 4, None, A.arith_shift_right, None, ["pidx"], ["ggi"])
-    ms(T.fx[:], 1.0, ["cum", "fg"])
+    ts(P15, T.pidx[:], 15.0, None, A.mult, None, ["pidx"], ["p15"])
     cp(PM, T.pmi[:], ["pmi"], ["pm"])
     cp(GM, T.gmi[:], ["gmi"], ["gm"])
     cp(GP, T.ggi[:], ["ggi"], ["gp"])
+    cp(PP, T.pidx[:], ["pidx"], ["pp"])
     ms(T.fx[:, 0:1], 0.0, ["cum"])
     ts(T.eq[:], T.ci[:], PM, None, A.is_equal, None, ["ci", "pm"], ["eq"])
+    ts(T.b8[:], T.vc[:], P15, None, A.is_equal, None, ["vc", "p15"], ["b8"])
     ts(mat("blk"), T.gx[:], GP, None, A.is_equal, None, ["gx", "gp"], ["blk"])
-    ts(VOFF, GP, -16.0 * NC, None, A.mult, None, ["gp"], ["voff"])
     tt(T.wt[:, 1:16], T.eq[:, 0:15], T.eq[:, 1:16], A.subtract, ["eq"], ["wt"])
-    ts(T.b8[0:32, :], T.vd[0:32, :], 0.0, None, A.is_equal, None, ["vd"], ["b8"])
-    cp(T.snu[:], T.sni[:], ["sni"], ["snu"])
+    ts(VOFF, PM, float(NC), PP, A.mult, A.add, ["pm", "pp"], ["voff"])
     ts(T.ta[:], vb, 0.0, None, A.is_ge, None, ["vc"], ["ta"])
-    ts(T.o1[:], T.vc[:], PM, 0.0, A.add, A.is_equal, ["vc", "pm"], ["o1"])
     cp(E15, T.eq[:, 15:16], ["eq"], ["e15c"])
-    ts(mat("one"), vb, 0.0, None, A.is_equal, None, ["vc"], ["one"])
-    tt(T.tb[:], T.ta[:], mat("blk"), A.mult, ["ta", "blk"], ["tb"])
-    ts(WL, E15, 17.0, -1.0, A.mult, A.add, ["e15c"], ["wl"])
-    ts(T.vj[:], T.vi[:], VOFF, None, A.add, None, ["vi", "voff"], ["vj"])
+    cp(T.snu[:], T.sni[:], ["sni"], ["snu"])
     cp(T.flb[0:8, :], T.fli[0:8, :], ["fli"], ["flb"])
     mms([(FS, lane(T.b8, l, 8), T.flb[0:8, l:V:16]) for l in range(16)], ["b8", "flb"], ["#7"])
+
+    def pick_d(src, d):
+        ac(T.sbf[:, GS * (d - 1):GS * d], W[src][:, 0:V].indirect(T.snu[:, 32 * (d - 1):32 * d]), F.Identity,
+           ["w%down" % src, "snu"], ["sbf%d" % d])
+
+    def send_d(dstw, ds):
+        k = ne // len(ds)
+        send([(peer(d), j * k, j * k + k, T.sbf[:, GS * (d - 1):GS * d], W[dstw][:, V + GS * (d - 1):V + GS * d])
+              for j, d in enumerate(ds)], "aw%d" % dstw, ["sbf%d" % d for d in ds])
+
+    for d in range(1, N):
+        pick_d(0, d)
+    send_d(0, [1])
+    send_d(0, [2, 3])
+    ts(T.vj[:], T.vc[:, 16:16 + NC], VOFF, None, A.add, None, ["vc", "voff"], ["vj"])
+    tt(T.tb[:], T.ta[:], mat("blk"), A.mult, ["ta", "blk"], ["tb"])
     ts(T.ya[:, 0:7], T.ci[:, 0:7], 16.0, PM, A.mult, A.add, ["ci", "pm"], ["ya"])
     ms(T.dua[:], 0.0, ["dua"])
     cp(mat("tri"), T.tb[:], ["tb"], ["tri"])
     ts(mat("e15"), vb, 0.0, E15, A.is_equal, A.mult, ["vc", "e15c"], ["e15"])
     ts(T.dua[:, 7:14], T.ya[:, 0:7], -1.0 / 256.0, -0.5, A.mult, A.add, ["ya"], ["dua"])
     ms(T.mat[:, 128 * MATS.index("tri") + 15:128 * MATS.index("tri") + 128:16], 0.0, ["tri"])
-    ts(DEC, E15, -1.0, None, A.add, None, ["e15c"], ["decc"])
-    fill(T.labi[:, V:TW], CAP, NP - 1, ["labpad"], False)
+    ts(T.crow[:], T.vc[:, 16:16 + NC], PP, None, A.add, None, ["vc", "pp"], ["crow"])
+    ts(T.o1[:], T.vc[:], PM, 0.0, A.add, A.is_equal, ["vc", "pm"], ["o1"])
+    ts(mat("one"), vb, 0.0, None, A.is_equal, None, ["vc"], ["one"])
     dma("y", T.labi[15:128:16, :], T.vj[:], ["vj", "labpad"], ["lab15", "labpad"])
-
-    def pick_d(src, d):
-        a = GS * (d - 1)
-        ac(T.sbf[:, a:a + GS], W[src][:, 0:V].indirect(T.snu[:, 32 * (d - 1):32 * d]), F.Identity,
-           ["w%down" % src, "snu"], ["sbf%d" % d])
-
-    def send_d(dstw, d):
-        a = GS * (d - 1)
-        send([(peer(d), 0, ne, T.sbf[:, a:a + GS], W[dstw][:, V + a:V + a + GS])], "aw%d" % dstw, ["sbf%d" % d])
-
-    for d in range(1, N):
-        pick_d(0, d)
-        send_d(0, d)
-    dma("y", T.nbw[:, 0:V], T.nb[:], ["sbf3"], ["nbw"])
-    dma("y", T.ndw[:, 0:V], T.nd[:], [], ["ndw"])
     fill(T.nbw[:, V:TW], CAP, NP - 1, ["nbpad"], False)
+    dma("y", T.nbw[:, 0:V], T.nb[:], ["nbpad"], ["nbw"])
+    dma("y", T.ndw[:, 0:V], T.nd[:], [], ["ndw"])
     fill(T.gs[:, V:2 * V], V, 0, ["gs"])
     dma("y", T.gv[:, 0:V], T.gs[:, V:2 * V], ["gs"], ["gvown"])
     dma("y", T.gs[:, 0:V], T.gs[:, V:2 * V], ["gs"], ["gsown"])
@@ -263,43 +263,54 @@ def rank_program(g, core, T, topo):
     dma("y", T.ov[0:128:16, :], T.gs[0:128:8, V:2 * V], ["gs"], ["ov"])
     dma("y", T.ow[0:128:16, :], T.gs[0:128:8, V:2 * V], ["gs"], ["ow"])
 
-    for i in range(1, 16):
-        ac(mat("d%d" % i), mat("blk"), F.Identity, ["blk", "wt"], ["d%d" % i], scale=T.wt[:, i:i + 1])
-    ac(mat("l14"), mat("blk"), F.Identity, ["blk", "eq"], ["l14"], scale=T.eq[:, 14:15])
     DM = ["d%d" % i for i in range(1, 16)] + ["l14", "p512", "ones"]
 
-    def late_constants(step):
-        if step == 0:
-            ts(T.ta[:], vb, 0.0, 4095.0, A.is_equal, A.mult, ["vc"], ["ta"])
-            ts(T.dec[:], T.ones[:], DEC, None, A.mult, None, ["ones", "decc"], ["dec"])
-            ts(MINS, E15, 999.0, 1.0, A.mult, A.add, ["e15c"], ["mins"])
-            tt(mat("trs"), T.tb[:], T.ta[:], A.add, ["ta", "tb"], ["trs"])
-            ts(T.o2[:], T.o1[:], WL, None, A.mult, None, ["o1", "wl"], ["o2"])
+    spare = [lambda: ts(DEC, E15, -1.0, None, A.add, None, ["e15c"], ["decc"]),
+             lambda: ms(T.hw[:, 0:CAP], 0.0, ["hw"]),
+             lambda: ts(WL, E15, 17.0, -1.0, A.mult, A.add, ["e15c"], ["wl"]),
+             lambda: ts(T.ta[:], vb, 0.0, 4095.0, A.is_equal, A.mult, ["vc"], ["ta"]),
+             lambda: ts(T.dec[:], T.ones[:], DEC, None, A.mult, None, ["ones", "decc"], ["dec"]),
+             lambda: ts(MINS, E15, 999.0, 1.0, A.mult, A.add, ["e15c"], ["mins"]),
+             lambda: ts(T.o2[:], T.o1[:], WL, None, A.mult, None, ["o1", "wl"], ["o2"]),
+             lambda: ts(KD, PM, -8.0, 1.0 / 32.0, A.add, A.mult, ["pm"], ["kdc"]),
+             lambda: tt(mat("trs"), T.tb[:], T.ta[:], A.add, ["ta", "tb"], ["trs"])]
+    spare += [lambda i=i: ts(mat("d%d" % i), mat("blk"), T.wt[:, i:i + 1], None, A.mult, None, ["blk", "wt"], ["d%d" % i])
+              for i in range(1, 9)]
+    spare += [lambda: ts(GB, PM, 32.0, GM, A.mult, A.add, ["pm", "gm"], ["gb"]),
+              lambda: ts(T.b3[:], T.vc[:], 0.0, -1.0, A.is_equal, A.mult, ["vc"], ["b3"]),
+              lambda: ts(T.gl[:], T.ci[:], GB, None, A.add, None, ["ci", "gb"], ["gl"])]
+
+    def between(n):
+        for _ in range(min(n, len(spare))):
+            spare.pop(0)()
+
+    def scalar_constants():
+        scaled(T.ldw[:, V:TW], T.ones[:], 255.0, ["ones"], ["ldpad"])
+        for i in range(9, 16):
+            scaled(mat("d%d" % i), mat("blk"), T.wt[:, i:i + 1], ["blk", "wt"], ["d%d" % i])
+        scaled(mat("l14"), mat("blk"), T.eq[:, 14:15], ["blk", "eq"], ["l14"])
+        scaled(mat("p512"), mat("one"), 512.0, ["one"], ["p512"])
+        scaled(W[0][:, 3088:WW], T.ones[:, 0:16], 255.0, ["ones"], ["w0none"])
+        scaled(T.ndw[:, V:TW], T.ones[:], 255.0, ["ones"], ["ndpad"])
+        scaled(mat("l15"), mat("blk"), E15, ["blk", "e15c"], ["l15"])
+        scaled(mat("neg"), mat("one"), -1.0, ["one"], ["neg"])
+        scaled(mat("n15"), mat("l15"), -1.0, ["l15"], ["n15"])
+        scaled(mat("n512"), mat("one"), -512.0, ["one"], ["n512"])
+        scaled(mat("sum4k"), mat("blk"), -4096.0, ["blk"], ["sum4k"])
+        scaled(mat("kd"), mat("one"), KD, ["one", "kdc"], ["kd"])
+
+    def slot_columns(step):
         if step == 1:
-            ms(T.ldw[:, V:TW], 255.0, ["ldpad"])
-            ts(mat("p512"), vb, 0.0, 512.0, A.is_equal, A.mult, ["vc"], ["p512"])
-            ts(KD, PM, -8.0, 1.0 / 32.0, A.add, A.mult, ["pm"], ["kdc"])
-            ts(GB, PM, 32.0, GM, A.mult, A.add, ["pm", "gm"], ["gb"])
-            ts(mat("l15"), mat("blk"), E15, None, A.mult, None, ["blk", "e15c"], ["l15"])
-            ts(mat("n15"), mat("blk"), E15, -1.0, A.mult, A.mult, ["blk", "e15c"], ["n15"])
-        if step == 2:
-            ms(W[0][:, 3088:WW], 255.0, ["w0none"])
-            ms(T.ndw[:, V:TW], 255.0, ["ndpad"])
-            ts(mat("neg"), vb, 0.0, -1.0, A.is_equal, A.mult, ["vc"], ["neg"])
-            ts(mat("n512"), vb, 0.0, -512.0, A.is_equal, A.mult, ["vc"], ["n512"])
-            ts(mat("kd"), vb, 0.0, KD, A.is_equal, A.mult, ["vc", "kdc"], ["kd"])
-            ts(mat("sum4k"), mat("blk"), -4096.0, None, A.mult, None, ["blk"], ["sum4k"])
-            ts(T.gl[:], T.ci[:], GB, None, A.add, None, ["ci", "gb"], ["gl"])
-            ts(T.idf[:], vb, 0.0, None, A.is_equal, None, ["vc"], ["idf"])
-            ts(T.b3[:], T.vc[:], 0.0, -1.0, A.is_equal, A.mult, ["vc"], ["b3"])
-            ts(T.sa[:], T.sr[:], 15, None, A.bitwise_and, None, ["sr"], ["sa"])
-            ts(T.sb[:], T.sr[:], 4, None, A.arith_shift_right, None, ["sr"], ["sb"])
-            ts(T.b2[:], T.b3[:], T.eq[:, 0:1], None, A.mult, None, ["b3", "eq"], ["b2"])
-            ts(T.sc[:], T.sa[:], 96.0, None, A.mult, None, ["sa"], ["sc"])
             ms(T.k0[:, 0:256:16], -256.75, ["k0"])
-            ms(T.y2[:], 0.0, ["y2"])
+        if step == 2:
+            ts(T.sa[:], T.sr[:], 15, None, A.bitwise_and, None, ["sr"], ["sa"])
+        if step == 3:
+            ts(T.sb[:], T.sr[:], 4, None, A.arith_shift_right, None, ["sr"], ["sb"])
+        if step == 4:
+            ts(T.sc[:], T.sa[:], 96.0, None, A.mult, None, ["sa"], ["sc"])
+        if step == 5:
             tt(T.sd[:], T.sc[:], T.sb[:], A.add, ["sc", "sb"], ["sd"])
-            ms(T.r2[:], 3328.0, ["r2"])
+        if step == 6:
             cp(T.lst[:], T.sd[:], ["sd"], ["lst"])
 
     for t in range(RO):
@@ -314,50 +325,64 @@ def rank_program(g, core, T, topo):
             tt(FG96, T.two[:], FS, A.is_ge, ["two", "#7"], ["fg"])
         else:
             ts(FG96, FS, 0.5, None, A.is_ge, None, ["#7"], ["fg"])
+        between(1)
         scan(T.fx[:, 1:NC], T.fx[:, NC:2 * NC - 1], T.fx[:, NC:2 * NC - 1], A.add, A.max, ["fg"], ["cum"])
         mms([(CI, mat("tri"), FG), (CI, mat("e15"), T.crow[:])], ["tri", "e15", "fg", "crow"], ["#6"])
         mms([(AP, mat("one"), T.dua[:, 0:14])] + [(AP, lane(T.o1, l), T.fx[:, l:2 * NC:16]) for l in range(16)],
             ["one", "dua", "o1", "cum", "fg"], ["#7"])
         ac(T.cis[:], CI, F.Identity, ["#6"], ["cis"])
+        between(6)
+        if t > 0:
+            tt(T.labf[:].indirect(T.tl[:]), T.lab32[:], T.d1[:], A.add, ["lab32", "d1", "tl"], ["labf"])
+        if last:
+            dma("y", T.yl[:], T.labf[:, 0:V], ["labf", wn + "g"], ["yl"])
+        ts(T.yb[:, 0:7], ps[:, b7 + 135:b7 + 142], -4096.0, None, A.mult, None, ["#7"], ["yb"])
+        between(1)
+        tt(T.yc[:, 0:7], ps[:, b7 + 128:b7 + 135], T.yb[:, 0:7], A.max, ["#7", "yb"], ["yc"])
+        between(1)
         if t == 0:
-            late_constants(0)
-        elif not last:
-            ms(T.y2[:, c - 1:256:16], 0.0, ["y2"])
+            scalar_constants()
         if not last:
             mms([(CG, mat("blk"), T.fx[:, 0:96]), (CG, mat("trs"), FG96)], ["blk", "trs", "cum", "fg"], ["#6"])
-        ts(T.yb[:, 0:7], ps[:, b7 + 135:b7 + 142], -4096.0, None, A.mult, None, ["#7"], ["yb"])
-        tt(T.yc[:, 0:7], ps[:, b7 + 128:b7 + 135], T.yb[:, 0:7], A.max, ["#7", "yb"], ["yc"])
         cp(T.off[:, 0:7], T.yc[:, 0:7], ["yc"], ["off"])
+        between(1)
         cp(T.hw[:].indirect(T.off[:, 0:7]), T.cis[:], ["off", "cis"], ["hw"])
+        between(1)
         scan(T.hg[:], T.dec[:], T.hw[:, 0:CAP], A.add, A.max, ["dec", "hw"], ["hg"])
+        between(1)
         ts(T.hm[:], T.hg[:], MINS, None, A.min, None, ["hg", "mins"], ["hm"])
         mms([(LP, lane(T.o2, l), T.hm[:, l:CAP:16]) for l in range(16)], ["o2", "hm"], ["#7"])
         if not last:
             fill(T.hw[:, 0:CAP], CAP, 0, ["hw"])
             ts(T.rem[:], CG, 4096.0 + CAP - 0.5, 0.9 * STAMP[t], A.is_lt, A.mult, ["#6"], ["rem"])
-        if t == 0:
-            late_constants(1)
-        elif not last:
+        between(5)
+        if 0 < t < RO - 1:
             ms(T.y1[:, c - 1:256:16], 0.0, ["y1"])
+            ms(T.y2[:, c - 1:256:16], 0.0, ["y2"])
         ts(T.tl[:], LP, 15.0, None, A.add, None, ["#7"], ["tl"])
+        between(1)
         L = T.tl[:]
         ac(T.ldt[:], T.ldw[:].indirect(L), F.Identity, ["ldw", "ldpad", "tl"], ["ldt"])
         if t == 0:
-            cp(T.labu[:], T.labi[:].indirect(L), ["labi", "labpad", "tl"], ["labu"])
-            late_constants(2)
+            cp(T.labu[:], T.labi[:].indirect(L), ["labi", "labpad", "tl"], ["labu0", "labu1"])
+            between(2)
+            fill(T.y2[:], 256, 0, ["y2"])
+            fill(T.k0[:], 256, -1000, ["k0"])
             iota(T.r1[:], [[1, 272]], -224, 0, ["r1"])
+            fill(T.r2[:], 272, 3328, ["r2"])
             for j in range(RO - 1):
                 fill(T.st[:, 256 * j:256 * j + 256], 256, STAMP[j], ["st%d" % j])
             comp("g", lambda: g.affine_select(T.labf[:], T.labi[:], [[0, TW]], A.is_ge, 0.0, 1, 0),
                  ["labi", "labpad"], ["labf"])
         else:
-            cp(T.labu[:], T.labf[:].indirect(L), ["labf", "tl"], ["labu"])
+            cp(T.labu[:, 0:128], T.labf[:].indirect(T.tl[:, 0:8]), ["labf", "tl"], ["labu0"])
+            cp(T.labu[:, 128:256], T.labf[:].indirect(T.tl[:, 8:16]), ["labf", "tl"], ["labu1"])
         if t == 1:
             fill(T.lo[:], TW, NP - 1, ["lo"])
         win = W[t][:, 0:NP]
 
         def gather(q, h0, h1):
-            lu, nm = (T.labu, "labu") if h0 < 16 else (T.nbu, "nbu")
+            lu, nm = (T.labu, "labu%d" % (h0 // 8)) if h0 < 16 else (T.nbu, "nbu")
             o = lu[:, 16 * (h0 % 16):16 * (h0 % 16 + h1 - h0)]
             out = T.gt[:, 256 * h0:256 * h1]
             wr = ["gt%d" % h for h in range(h0, h1)]
@@ -380,6 +405,9 @@ def rank_program(g, core, T, topo):
                  sorted(set("#%d" % (h // 2 % 6) for h in range(h0, h1))) + ["gt%d" % h for h in range(h0, h1)],
                  ["sn%d" % h for h in range(h0, h1)])
 
+        def neighbours():
+            cp(T.nbu[:], T.nbw[:].indirect(L), ["nbw", "nbpad", "tl"], ["nbu"])
+
         gtl = ["gt%d" % h for h in range(16)]
         snl, snn = ["sn%d" % h for h in range(16)], ["sn%d" % h for h in range(16, 32)]
         old, thr, sc = T.gt[:, 15:4096:16], T.sn[:, 15:4096:16], T.sn[:, 4096 + 15:8192:16]
@@ -387,6 +415,8 @@ def rank_program(g, core, T, topo):
             diffs(u)
         gather("s", 4, 8)
         gather("v", 0, 4)
+        if t > 0:
+            neighbours()
         gather("s", 8, 12)
         ac(T.ndt[:], T.ndw[:].indirect(L), F.Identity, ["ndw", "ndpad", "tl"], ["ndt"])
         gather("s", 12, 16)
@@ -394,11 +424,11 @@ def rank_program(g, core, T, topo):
         diffs(6)
         diffs(7)
         least(4, 8)
-        cp(T.nbu[:], T.nbw[:].indirect(L), ["nbw", "nbpad", "tl"], ["nbu"])
+        if t == 0:
+            neighbours()
         diffs(8)
         diffs(9)
-        if XV:
-            gather("v", 16, 16 + XV)
+        gather("v", 16, 16 + XV)
         least(8, 12)
         diffs(10)
         diffs(11)
@@ -454,21 +484,28 @@ def rank_program(g, core, T, topo):
         tt(T.zz[:], T.nb32[:], ZW, A.max, ["nb32", "nb32b", "#4", "#5"], ["zz"])
         tr32(T.tt[:, 0:256], T.zz[:, 0:256], ["zz"], ["tt0"])
         tr32(T.tt[:, 256:512], T.zz[:, 16:272], ["zz"], ["tt1"])
-        cp(T.xo[:, 0:128], T.tt[:].indirect(T.gl[:, 0:8]), ["tt0", "tt1", "gl"], ["xo0"])
-        cp(T.xo[:, 128:256], T.tt[:].indirect(T.gl[:, 8:16]), ["tt0", "tt1", "gl"], ["xo1"])
+
+        def lists(a, b):
+            cp(T.xo[:, 16 * a:16 * b], T.tt[:].indirect(T.gl[:, a:b]), ["tt0", "tt1", "gl"], ["xo%d" % i for i in range(a, b)])
         stamp = T.st[:, 256 * t:256 * (t + 1)]
-        new_d()
-        for i in range(8, 16):
-            cp(T.gv[:].indirect(T.xo[:, 16 * i:16 * i + 16]), stamp, ["xo1", "st%d" % t], ["gv", "gvown"])
-        for i in range(8):
-            ac(T.gs[:].indirect(T.xo[:, 16 * i:16 * i + 16]), stamp, F.Silu, ["xo0", "st%d" % t], ["gs", "gsown"])
-            if i == 2:
-                pick_d(t, 1)
-                send_d(t + 1, 1)
-            if i == 4:
+        lists(0, 4)
+        for j in range(8):
+            i = 4 * (j // 2) + 2 + j % 2
+            cp(T.gv[:].indirect(T.xo[:, 16 * i:16 * i + 16]), stamp, ["xo%d" % i, "st%d" % t], ["gv", "gvown"])
+            if j < 3:
+                lists(4 * j + 4, 4 * j + 8)
+            if t == 0:
+                slot_columns(j)
+        for j in range(8):
+            i = 4 * (j // 2) + j % 2
+            ac(T.gs[:].indirect(T.xo[:, 16 * i:16 * i + 16]), stamp, F.Silu, ["xo%d" % i, "st%d" % t], ["gs", "gsown"])
+            if j == 0 and t == 0:
+                scaled(T.idf[:], mat("one"), 1.0, ["one"], ["idf"])
+            if j == 1 and t == 0:
+                scaled(T.b2[:], T.b3[:], T.eq[:, 0:1], ["b3", "eq"], ["b2"])
+            if j == 4:
                 ac(W[t + 1][:, 3072:WW], W[0][:, 3072:WW], F.Identity, ["w0rt", "w0none"],
                    ["w%drt" % (t + 1), "w%dnone" % (t + 1)])
-        dma("y", W[t + 1][:, 0:V], W[t][:, 0:V], [wn + "own"], ["w%down" % (t + 1)])
         R = T["fr%d" % t]
         for h in range(2):
             a = V + GS * h
@@ -476,16 +513,19 @@ def rank_program(g, core, T, topo):
                ["lst", "gv", "gs", "ov"], ["ov%d" % h])
             ac(T.ow[:, V * h:V * h + V].indirect(T.lst[:, 64:96]), (T.gs, T.gv)[h][:, V + 2 * GS:2 * V], F.Silu,
                ["lst", ("gs", "gv")[h], "ow"], ["ow%d" % h])
-            dma("y", T.xf[:, 192 * h + 96:192 * h + 192], T.ow[0:128:16, V * h:V * h + V], ["ow%d" % h], ["xw%d" % h])
+            dma("ys"[h], T.xf[:, 192 * h + 96:192 * h + 192], T.ow[0:128:16, V * h:V * h + V], ["ow%d" % h], ["xw%d" % h])
             dma("y", T.xf[:, 192 * h:192 * h + 96], T.ov[0:128:16, V * h:V * h + V], ["ov%d" % h], ["xv%d" % h])
         for h in range(2):
             a = 192 * h
             send([(peer(-1 - h), 0, 2 * q4, T.xf[:, a:a + 96], R[:, a:a + 96]),
                   (peer(-3), 2 * q4, ne, T.xf[:, a + 96:a + 192], R[:, a + 96:a + 192])], "af%d%d" % (t, h),
                  ["xv%d" % h, "xw%d" % h])
-        for d in (2, 3):
+        new_d()
+        for d in range(1, N):
             pick_d(t, d)
-            send_d(t + 1, d)
+        send_d(t + 1, [1, 2])
+        send_d(t + 1, [3])
+        dma("y", W[t + 1][:, 0:V], W[t][:, 0:V], [wn + "own"], ["w%down" % (t + 1), "xv1"])
         mms([(FS, T.idf[:], T.rem[:], True, False)]
             + [(FS, lane(T.b2, l), T.gs[:, l:V:16], False, False) for l in range(16)], ["idf", "b2", "rem", "gs"], ["#7"])
         mms([(FS, lane(T.b2, l), T.gv[:, l:V:16], False, False) for l in range(16)], ["b2", "gv"], ["#7"])
@@ -496,9 +536,6 @@ def rank_program(g, core, T, topo):
         ts(T.y1[:, c:256:16], T.df[:], 32.0, 257.0 * 32.0 - 8.0, A.mult, A.add, ["df"], ["y1"])
         tt(T.ldw[:].indirect(L), T.ldt[:], T.d2[:], A.add, ["ldt", "d2", "tl"], ["ldw", "ldpad"])
         tr32(T.d1[:], T.y1[:], ["y1"], ["d1"])
-        tt(T.labf[:].indirect(L), T.lab32[:], T.d1[:], A.add, ["lab32", "d1", "tl"], ["labf"])
-        if t == RO - 2:
-            dma("y", T.yl[:], T.labf[:, 0:V], ["labf", "w%dg" % (t + 1)], ["yl"])
 
     num = {}
     for o in ops:

from concourse.bass import DstId, RemoteDMATransfer
from concourse.mybir import AluOpType, ActivationFunctionType

A = AluOpType
F = ActivationFunctionType
N, V, GS, CAP, RO = 4, 1536, 512, 256, 4
NP = V + 3 * GS + 17
WW = 3104
TW = V + CAP
NC = TW // 16
HW = 3840
GW = 3376
STAMP = (32.0, 256.0, 2048.0)
ROUND = 1.5 * 2.0 ** 23
XV = 2
CUTS, LAST = (20, 24, 28, 30, 31), (30, 31)
MATS = ["d%d" % i for i in range(1, 16)] + "l14 l15 n15 one neg p512 n512 kd sum4k tri e15 blk trs".split()

SCRATCH = {"ps": ("psum", [128, 4096], "float32")}
for names, width, kind in (
        ("nbw labi", TW, "int32"), ("labf lo", TW, "float32"), ("ndw ldw", TW, "bfloat16"),
        ("fli", V, "int32"), ("flb sbf", V, "bfloat16"), ("sni sr sa sb sc sd", 96, "int32"), ("snu lst", 96, "uint16"),
        ("off", 8, "uint16"), ("vj", NC, "int32"),
        ("rem two", 96, "float32"), ("xf", 384, "float32"), ("fx", 2 * NC, "bfloat16"), ("crow cis", NC, "bfloat16"),
        ("hw", HW, "bfloat16"), ("gv gs", GW, "float32"), ("ov ow", 3072, "float32"),
        ("gt sn", 8192, "bfloat16"), ("mat", len(MATS) * 128, "bfloat16"),
        ("vc b2 b3", 144, "float32"), ("o1 o2 b8", 144, "bfloat16"), ("gx idf ta tb", 128, "float32"),
        ("pidx pmi gmi ggi", 1, "int32"), ("col", 16, "float32"), ("ci eq wt df ya yb yc", 16, "float32"),
        ("dua", 16, "bfloat16"), ("gl", 16, "uint16"), ("tl", 16, "uint16"),
        ("r1 r2", 272, "bfloat16"), ("st", 768, "float32"), ("zz nb32", 272, "float32"), ("tt", 512, "float32"),
        ("labu nbu xo", 256, "uint16"), ("k0 lab32 kt ks y1 d1", 256, "float32"),
        ("ldt ndt up dm y2 d2 dec hg hm ones", 256, "bfloat16"),
        ("w0 w1 w2 w3", WW, "bfloat16"), ("fr0 fr1 fr2", 384, "float32")):
    for name in names.split():
        SCRATCH[name] = ("sbuf", [128, width], kind)

SEMAPHORES = (["qv", "qs", "qp", "qg", "alst"] + ["aw%d" % t for t in range(RO)]
              + ["af%d%d" % (t, h) for t in range(RO - 1) for h in range(2)]
              + ["dm%d" % i for i in range(48)] + ["rm%d" % i for i in range(24)])


def rank_program(g, core, T, topo):
    rank = T.rank_of(core)
    if rank is None:
        return
    Q = {"v": g.vector, "s": g.scalar, "p": g.tensor, "g": g, "y": g.sync}
    ops, lastw, readers = [], {}, {}
    cnt = {"dm": 0, "rm": 0}

    def add(q, kind, fn, rd, wr, sem=None, val=0):
        o = {"q": q, "kind": kind, "fn": fn, "sem": sem, "val": val, "need": False, "deps": []}
        dep = []
        for r in rd:
            if r in lastw:
                dep.append(lastw[r])
            if r[0] == "#":
                dep += [x for x in readers.get(r, []) if x["q"] != q]
        for w in wr:
            for x in ([lastw[w]] if w in lastw else []) + readers.get(w, []):
                if not (q == "p" and x["q"] == q):
                    dep.append(x)
        for x in dep:
            if all(x is not z for z in o["deps"]):
                o["deps"].append(x)
                x["need"] = True
        for r in rd:
            readers.setdefault(r, []).append(o)
        for w in wr:
            lastw[w] = o
            readers[w] = []
        ops.append(o)

    def comp(q, fn, rd, wr):
        add(q, "c", fn, rd, wr, "q" + q)

    def dmas(q, pairs, rd, wr):
        s = "dm%d" % cnt["dm"]
        cnt["dm"] += 1

        def fn():
            for out, in_ in pairs:
                Q[q].dma_start(out, in_).then_inc(T.sem[s], 16)
        add(q, "d", fn, rd, wr, s, 16 * len(pairs))

    def dma(q, out, in_, rd, wr):
        dmas(q, [(out, in_)], rd, wr)

    def arrival(sem, val, wr):
        add(None, "a", None, [], wr, sem, val)

    def peer(d):
        return T.cores[(rank + d) % N]

    def bits(dst, lo, hi):
        m = 0
        for e in topo.engines(core, dst)[lo:hi]:
            m |= 1 << e
        return m

    ne = len(topo.engines(core, peer(1)))
    q4 = ne // 4

    def send(parts, rsem, rd):
        s = "rm%d" % cnt["rm"]
        cnt["rm"] += 1

        def fn():
            if len(parts) == 1:
                dst, lo, hi, src, out = parts[0]
                rid, pid = topo.addr(dst)[0:2]
                g.remote_dma(out, src, T.sem[rsem], T.sem[s], pid, rid, bits(dst, lo, hi))
                return
            tr = []
            for dst, lo, hi, src, out in parts:
                rid, pid = topo.addr(dst)[0:2]
                tr.append(RemoteDMATransfer(dst_ids=[DstId(rid=rid, pnc=pid)], dma_engine_mask=bits(dst, lo, hi),
                                            remote_sem=T.sem[rsem], srcs=[src], dsts=[out], alu_op=0))
            g.remote_dma_fused(tr, local_sem=T.sem[s])
        add("g", "r", fn, rd, [], s, sum(p[2] - p[1] for p in parts))

    vec, act, pe = g.vector, g.scalar, g.tensor

    def ts(out, in0, s1, s2, op0, op1, rd, wr):
        if op1 is None:
            comp("v", lambda: vec.tensor_scalar(out, in0, s1, None, op0), rd, wr)
        else:
            comp("v", lambda: vec.tensor_scalar(out, in0, s1, s2, op0, op1), rd, wr)

    def tt(out, in0, in1, op, rd, wr):
        comp("v", lambda: vec.tensor_tensor(out, in0, in1, op), rd, wr)

    def cp(out, in_, rd, wr):
        comp("v", lambda: vec.tensor_copy(out, in_), rd, wr)

    def ms(ap, const, wr):
        comp("v", lambda: vec.memset(ap, const), [], wr)

    def tr32(out, in_, rd, wr):
        comp("v", lambda: vec.transpose(out, in_), rd, wr)

    def scan(out, d0, d1, op0, op1, rd, wr, first=0.0):
        comp("v", lambda: vec.tensor_tensor_scan(out, d0, d1, first, op0, op1), rd, wr)

    def ac(out, in_, func, rd, wr, **kw):
        comp("s", lambda: act.activation(out, in_, func, **kw), rd, wr)

    def scaled(out, src, scale, rd, wr):
        ac(out, src, F.Identity, rd, wr, scale=scale)

    def iota(out, pat, base, cm, wr, flt=True):
        if flt:
            comp("g", lambda: g.iota(out, pat, base, cm, allow_small_or_imprecise_dtypes=True), [], wr)
        else:
            comp("g", lambda: g.iota(out, pat, base, cm), [], wr)

    def fill(out, width, value, wr, flt=True):
        iota(out, [[0, width]], int(value), 0, wr, flt)

    def mms(lst, rd, wr):
        def fn():
            r = None
            for j, m in enumerate(lst):
                a, b = m[3:5] if len(m) > 3 else (j == 0, j == len(lst) - 1)
                r = pe.matmul(m[0], m[1], m[2], a, b)
            return r
        comp("p", fn, rd, wr)

    W = [T["w%d" % t] for t in range(RO)]
    ps = T.ps

    def mat(name):
        j = MATS.index(name)
        return T.mat[:, 128 * j:128 * (j + 1)]

    def lane(buf, l, rows=128):
        return buf[0:rows, 16 - l:144 - l]

    PM, GP, GB, KD, E15, WL, MINS, DEC, VOFF, GM, PP, P15 = [T.col[:, j:j + 1] for j in range(12)]
    FG, FG96 = T.fx[:, NC:2 * NC], T.fx[:, NC:NC + 96]
    b6, b7 = 6 * 512, 7 * 512
    TH, CI, CG = ps[:, b6:b6 + 256], ps[:, b6 + 256:b6 + 256 + NC], ps[:, b6 + 384:b6 + 480]
    FS, AP, LP = ps[:, b7:b7 + 96], ps[:, b7 + 128:b7 + 142], ps[:, b7 + 160:b7 + 176]
    DE, KEY = ps[:, 0:256], ps[:, 512:768]
    ZA, ZB, ZW = ps[:, 2304:2560], ps[:, 2560:2576], ps[:, 2304:2576]

    dma("s", T.sni[:], T.snd[:], [], ["sni"])
    dma("y", T.fli[0:8, :], T.fl[:], [], ["fli"])
    dma("y", W[0][:, 0:V], T.d0[:], [], ["w0own"])
    dmas("y", [(T.labi[a:a + 15, 0:V], T.lab[a:a + 15, :]) for a in range(0, 128, 16)], [], ["labi"])
    dma("s", W[0][:, 3072:3088], T.rt[:], [], ["w0rt"])
    dma("y", T.ldw[:, 0:V], T.ld[:], [], ["ldw"])
    for t in range(RO):
        arrival("aw%d" % t, 2 * ne, ["w%dg" % t])
    for t in range(RO - 1):
        for h in range(2):
            arrival("af%d%d" % (t, h), ne, ["fr%d%d" % (t, h)])
    arrival("alst", ne, ["sr"])

    iota(T.pidx[:], [[0, 1]], 0, 1, ["pidx"], False)
    iota(T.vc[:], [[1, 144]], -16, -1, ["vc"])
    iota(T.ci[:], [[1, 16]], 0, 0, ["ci"])
    iota(T.gx[:], [[1, 8], [0, 16]], 0, 0, ["gx"])
    fill(T.labi[:, V:TW], CAP, NP - 1, ["labpad"], False)
    send([(peer(1), 0, q4, T.sni[:, 0:32], T.sr[:, 0:32]), (peer(2), q4, 2 * q4, T.sni[:, 32:64], T.sr[:, 32:64]),
          (peer(3), 2 * q4, ne, T.sni[:, 64:96], T.sr[:, 64:96])], "alst", ["sni"])
    vb = T.vc[:, 16:144]

    ms(T.ones[:], 1.0, ["ones"])
    ms(T.fx[:], 1.0, ["cum", "fg"])
    ac(T.y1[:], T.ones[:], F.Silu, ["ones"], ["y1"], scale=0.0)
    ts(T.pmi[:], T.pidx[:], 15, None, A.bitwise_and, None, ["pidx"], ["pmi"])
    ts(T.gmi[:], T.pidx[:], 16, None, A.bitwise_and, None, ["pidx"], ["gmi"])
    ts(T.ggi[:], T.pidx[:], 4, None, A.arith_shift_right, None, ["pidx"], ["ggi"])
    ts(P15, T.pidx[:], 15.0, None, A.mult, None, ["pidx"], ["p15"])
    cp(PM, T.pmi[:], ["pmi"], ["pm"])
    cp(GM, T.gmi[:], ["gmi"], ["gm"])
    cp(GP, T.ggi[:], ["ggi"], ["gp"])
    cp(PP, T.pidx[:], ["pidx"], ["pp"])
    ms(T.fx[:, 0:1], 0.0, ["cum"])
    ts(T.eq[:], T.ci[:], PM, None, A.is_equal, None, ["ci", "pm"], ["eq"])
    ts(T.b8[:], T.vc[:], P15, None, A.is_equal, None, ["vc", "p15"], ["b8"])
    ts(mat("blk"), T.gx[:], GP, None, A.is_equal, None, ["gx", "gp"], ["blk"])
    tt(T.wt[:, 1:16], T.eq[:, 0:15], T.eq[:, 1:16], A.subtract, ["eq"], ["wt"])
    ts(VOFF, PM, float(NC), PP, A.mult, A.add, ["pm", "pp"], ["voff"])
    ts(T.ta[:], vb, 0.0, None, A.is_ge, None, ["vc"], ["ta"])
    cp(E15, T.eq[:, 15:16], ["eq"], ["e15c"])
    cp(T.snu[:], T.sni[:], ["sni"], ["snu"])
    cp(T.flb[0:8, :], T.fli[0:8, :], ["fli"], ["flb"])
    mms([(FS, lane(T.b8, l, 8), T.flb[0:8, l:V:16]) for l in range(16)], ["b8", "flb"], ["#7"])

    def pick_d(src, d):
        ac(T.sbf[:, GS * (d - 1):GS * d], W[src][:, 0:V].indirect(T.snu[:, 32 * (d - 1):32 * d]), F.Identity,
           ["w%down" % src, "snu"], ["sbf%d" % d])

    def send_d(dstw, ds):
        k = ne // len(ds)
        send([(peer(d), j * k, j * k + k, T.sbf[:, GS * (d - 1):GS * d], W[dstw][:, V + GS * (d - 1):V + GS * d])
              for j, d in enumerate(ds)], "aw%d" % dstw, ["sbf%d" % d for d in ds])

    for d in range(1, N):
        pick_d(0, d)
    send_d(0, [1])
    send_d(0, [2, 3])
    ts(T.vj[:], T.vc[:, 16:16 + NC], VOFF, None, A.add, None, ["vc", "voff"], ["vj"])
    tt(T.tb[:], T.ta[:], mat("blk"), A.mult, ["ta", "blk"], ["tb"])
    ts(T.ya[:, 0:7], T.ci[:, 0:7], 16.0, PM, A.mult, A.add, ["ci", "pm"], ["ya"])
    ms(T.dua[:], 0.0, ["dua"])
    cp(mat("tri"), T.tb[:], ["tb"], ["tri"])
    ts(mat("e15"), vb, 0.0, E15, A.is_equal, A.mult, ["vc", "e15c"], ["e15"])
    ts(T.dua[:, 7:14], T.ya[:, 0:7], -1.0 / 256.0, -0.5, A.mult, A.add, ["ya"], ["dua"])
    ms(T.mat[:, 128 * MATS.index("tri") + 15:128 * MATS.index("tri") + 128:16], 0.0, ["tri"])
    ts(T.crow[:], T.vc[:, 16:16 + NC], PP, None, A.add, None, ["vc", "pp"], ["crow"])
    ts(T.o1[:], T.vc[:], PM, 0.0, A.add, A.is_equal, ["vc", "pm"], ["o1"])
    ts(mat("one"), vb, 0.0, None, A.is_equal, None, ["vc"], ["one"])
    dma("y", T.labi[15:128:16, :], T.vj[:], ["vj", "labpad"], ["lab15", "labpad"])
    fill(T.nbw[:, V:TW], CAP, NP - 1, ["nbpad"], False)
    dma("y", T.nbw[:, 0:V], T.nb[:], ["nbpad"], ["nbw"])
    dma("y", T.ndw[:, 0:V], T.nd[:], [], ["ndw"])
    fill(T.gs[:, V:2 * V], V, 0, ["gs"])
    dma("y", T.gv[:, 0:V], T.gs[:, V:2 * V], ["gs"], ["gvown"])
    dma("y", T.gs[:, 0:V], T.gs[:, V:2 * V], ["gs"], ["gsown"])
    dma("y", T.gv[:, V:2 * V], T.gs[:, V:2 * V], ["gs"], ["gv"])
    dma("y", T.ov[0:128:16, :], T.gs[0:128:8, V:2 * V], ["gs"], ["ov"])
    dma("y", T.ow[0:128:16, :], T.gs[0:128:8, V:2 * V], ["gs"], ["ow"])

    DM = ["d%d" % i for i in range(1, 16)] + ["l14", "p512", "ones"]

    spare = [lambda: ts(DEC, E15, -1.0, None, A.add, None, ["e15c"], ["decc"]),
             lambda: ms(T.hw[:, 0:CAP], 0.0, ["hw"]),
             lambda: ts(WL, E15, 17.0, -1.0, A.mult, A.add, ["e15c"], ["wl"]),
             lambda: ts(T.ta[:], vb, 0.0, 4095.0, A.is_equal, A.mult, ["vc"], ["ta"]),
             lambda: ts(T.dec[:], T.ones[:], DEC, None, A.mult, None, ["ones", "decc"], ["dec"]),
             lambda: ts(MINS, E15, 999.0, 1.0, A.mult, A.add, ["e15c"], ["mins"]),
             lambda: ts(T.o2[:], T.o1[:], WL, None, A.mult, None, ["o1", "wl"], ["o2"]),
             lambda: ts(KD, PM, -8.0, 1.0 / 32.0, A.add, A.mult, ["pm"], ["kdc"]),
             lambda: tt(mat("trs"), T.tb[:], T.ta[:], A.add, ["ta", "tb"], ["trs"])]
    spare += [lambda i=i: ts(mat("d%d" % i), mat("blk"), T.wt[:, i:i + 1], None, A.mult, None, ["blk", "wt"], ["d%d" % i])
              for i in range(1, 9)]
    spare += [lambda: ts(GB, PM, 32.0, GM, A.mult, A.add, ["pm", "gm"], ["gb"]),
              lambda: ts(T.b3[:], T.vc[:], 0.0, -1.0, A.is_equal, A.mult, ["vc"], ["b3"]),
              lambda: ts(T.gl[:], T.ci[:], GB, None, A.add, None, ["ci", "gb"], ["gl"])]

    def between(n):
        for _ in range(min(n, len(spare))):
            spare.pop(0)()

    def scalar_constants():
        scaled(T.ldw[:, V:TW], T.ones[:], 255.0, ["ones"], ["ldpad"])
        for i in range(9, 16):
            scaled(mat("d%d" % i), mat("blk"), T.wt[:, i:i + 1], ["blk", "wt"], ["d%d" % i])
        scaled(mat("l14"), mat("blk"), T.eq[:, 14:15], ["blk", "eq"], ["l14"])
        scaled(mat("p512"), mat("one"), 512.0, ["one"], ["p512"])
        scaled(W[0][:, 3088:WW], T.ones[:, 0:16], 255.0, ["ones"], ["w0none"])
        scaled(T.ndw[:, V:TW], T.ones[:], 255.0, ["ones"], ["ndpad"])
        scaled(mat("l15"), mat("blk"), E15, ["blk", "e15c"], ["l15"])
        scaled(mat("neg"), mat("one"), -1.0, ["one"], ["neg"])
        scaled(mat("n15"), mat("l15"), -1.0, ["l15"], ["n15"])
        scaled(mat("n512"), mat("one"), -512.0, ["one"], ["n512"])
        scaled(mat("sum4k"), mat("blk"), -4096.0, ["blk"], ["sum4k"])
        scaled(mat("kd"), mat("one"), KD, ["one", "kdc"], ["kd"])

    def slot_columns(step):
        if step == 1:
            ms(T.k0[:, 0:256:16], -256.75, ["k0"])
        if step == 2:
            ts(T.sa[:], T.sr[:], 15, None, A.bitwise_and, None, ["sr"], ["sa"])
        if step == 3:
            ts(T.sb[:], T.sr[:], 4, None, A.arith_shift_right, None, ["sr"], ["sb"])
        if step == 4:
            ts(T.sc[:], T.sa[:], 96.0, None, A.mult, None, ["sa"], ["sc"])
        if step == 5:
            tt(T.sd[:], T.sc[:], T.sb[:], A.add, ["sc", "sb"], ["sd"])
        if step == 6:
            cp(T.lst[:], T.sd[:], ["sd"], ["lst"])

    for t in range(RO):
        last = t == RO - 1
        c = 12 + t
        wn = "w%d" % t
        wall = [wn + "own", wn + "g", wn + "rt", wn + "none"]
        if t > 0:
            R = T["fr%d" % (t - 1)]
            mms([(FS, lane(T.b3, 0), R[:, 96 * j:96 * j + 96], False, j == 1) for j in range(2)], ["b3", "fr%d0" % (t - 1)], ["#7"])
            tt(T.two[:], R[:, 192:288], R[:, 288:384], A.add, ["fr%d1" % (t - 1)], ["two"])
            tt(FG96, T.two[:], FS, A.is_ge, ["two", "#7"], ["fg"])
        else:
            ts(FG96, FS, 0.5, None, A.is_ge, None, ["#7"], ["fg"])
        between(1)
        scan(T.fx[:, 1:NC], T.fx[:, NC:2 * NC - 1], T.fx[:, NC:2 * NC - 1], A.add, A.max, ["fg"], ["cum"])
        mms([(CI, mat("tri"), FG), (CI, mat("e15"), T.crow[:])], ["tri", "e15", "fg", "crow"], ["#6"])
        mms([(AP, mat("one"), T.dua[:, 0:14])] + [(AP, lane(T.o1, l), T.fx[:, l:2 * NC:16]) for l in range(16)],
            ["one", "dua", "o1", "cum", "fg"], ["#7"])
        ac(T.cis[:], CI, F.Identity, ["#6"], ["cis"])
        between(6)
        if t > 0:
            tt(T.labf[:].indirect(T.tl[:]), T.lab32[:], T.d1[:], A.add, ["lab32", "d1", "tl"], ["labf"])
        if last:
            dma("y", T.yl[:], T.labf[:, 0:V], ["labf", wn + "g"], ["yl"])
        ts(T.yb[:, 0:7], ps[:, b7 + 135:b7 + 142], -4096.0, None, A.mult, None, ["#7"], ["yb"])
        between(1)
        tt(T.yc[:, 0:7], ps[:, b7 + 128:b7 + 135], T.yb[:, 0:7], A.max, ["#7", "yb"], ["yc"])
        between(1)
        if t == 0:
            scalar_constants()
        if not last:
            mms([(CG, mat("blk"), T.fx[:, 0:96]), (CG, mat("trs"), FG96)], ["blk", "trs", "cum", "fg"], ["#6"])
        cp(T.off[:, 0:7], T.yc[:, 0:7], ["yc"], ["off"])
        between(1)
        cp(T.hw[:].indirect(T.off[:, 0:7]), T.cis[:], ["off", "cis"], ["hw"])
        between(1)
        scan(T.hg[:], T.dec[:], T.hw[:, 0:CAP], A.add, A.max, ["dec", "hw"], ["hg"])
        between(1)
        ts(T.hm[:], T.hg[:], MINS, None, A.min, None, ["hg", "mins"], ["hm"])
        mms([(LP, lane(T.o2, l), T.hm[:, l:CAP:16]) for l in range(16)], ["o2", "hm"], ["#7"])
        if not last:
            fill(T.hw[:, 0:CAP], CAP, 0, ["hw"])
            ts(T.rem[:], CG, 4096.0 + CAP - 0.5, 0.9 * STAMP[t], A.is_lt, A.mult, ["#6"], ["rem"])
        between(5)
        if 0 < t < RO - 1:
            ms(T.y1[:, c - 1:256:16], 0.0, ["y1"])
            ms(T.y2[:, c - 1:256:16], 0.0, ["y2"])
        ts(T.tl[:], LP, 15.0, None, A.add, None, ["#7"], ["tl"])
        between(1)
        L = T.tl[:]
        ac(T.ldt[:], T.ldw[:].indirect(L), F.Identity, ["ldw", "ldpad", "tl"], ["ldt"])
        if t == 0:
            cp(T.labu[:], T.labi[:].indirect(L), ["labi", "labpad", "tl"], ["labu0", "labu1"])
            between(2)
            fill(T.y2[:], 256, 0, ["y2"])
            fill(T.k0[:], 256, -1000, ["k0"])
            iota(T.r1[:], [[1, 272]], -224, 0, ["r1"])
            fill(T.r2[:], 272, 3328, ["r2"])
            for j in range(RO - 1):
                fill(T.st[:, 256 * j:256 * j + 256], 256, STAMP[j], ["st%d" % j])
            comp("g", lambda: g.affine_select(T.labf[:], T.labi[:], [[0, TW]], A.is_ge, 0.0, 1, 0),
                 ["labi", "labpad"], ["labf"])
        else:
            cp(T.labu[:, 0:128], T.labf[:].indirect(T.tl[:, 0:8]), ["labf", "tl"], ["labu0"])
            cp(T.labu[:, 128:256], T.labf[:].indirect(T.tl[:, 8:16]), ["labf", "tl"], ["labu1"])
        if t == 1:
            fill(T.lo[:], TW, NP - 1, ["lo"])
        win = W[t][:, 0:NP]

        def gather(q, h0, h1):
            lu, nm = (T.labu, "labu%d" % (h0 // 8)) if h0 < 16 else (T.nbu, "nbu")
            o = lu[:, 16 * (h0 % 16):16 * (h0 % 16 + h1 - h0)]
            out = T.gt[:, 256 * h0:256 * h1]
            wr = ["gt%d" % h for h in range(h0, h1)]
            if q == "v":
                cp(out, win.indirect(o), wall + [nm], wr)
            else:
                ac(out, win.indirect(o), F.Identity, wall + [nm], wr)

        def diffs(u):
            b = u % 6
            src = (T.ldt if u < 8 else T.ndt)[:, 32 * (u % 8):32 * (u % 8) + 32]
            lst = [(ps[:, 512 * b:512 * b + 512:16], mat("p512"), T.ones[:, 0:32], True, True)] if u < 6 else []
            for i in range(1, 16):
                lst.append((ps[:, 512 * b + i:512 * b + 512:16], mat("l14" if u < 8 and i == 15 else "d%d" % i), src, True, True))
            mms(lst, DM + ["ldt" if u < 8 else "ndt"], ["#%d" % b])

        def least(h0, h1):
            b = h0 % 12
            scan(T.sn[:, 256 * h0:256 * h1], ps[:, 256 * b:256 * (b + h1 - h0)], T.gt[:, 256 * h0:256 * h1], A.add, A.min,
                 sorted(set("#%d" % (h // 2 % 6) for h in range(h0, h1))) + ["gt%d" % h for h in range(h0, h1)],
                 ["sn%d" % h for h in range(h0, h1)])

        def neighbours():
            cp(T.nbu[:], T.nbw[:].indirect(L), ["nbw", "nbpad", "tl"], ["nbu"])

        gtl = ["gt%d" % h for h in range(16)]
        snl, snn = ["sn%d" % h for h in range(16)], ["sn%d" % h for h in range(16, 32)]
        old, thr, sc = T.gt[:, 15:4096:16], T.sn[:, 15:4096:16], T.sn[:, 4096 + 15:8192:16]
        for u in range(6):
            diffs(u)
        gather("s", 4, 8)
        gather("v", 0, 4)
        if t > 0:
            neighbours()
        gather("s", 8, 12)
        ac(T.ndt[:], T.ndw[:].indirect(L), F.Identity, ["ndw", "ndpad", "tl"], ["ndt"])
        gather("s", 12, 16)
        least(0, 4)
        diffs(6)
        diffs(7)
        least(4, 8)
        if t == 0:
            neighbours()
        diffs(8)
        diffs(9)
        gather("v", 16, 16 + XV)
        least(8, 12)
        diffs(10)
        diffs(11)
        for a, b in zip((16 + XV,) + CUTS, CUTS + (32,)):
            gather("s", a, b)
        if not last:
            ac(T.nb32[:, 0:256], T.nbw[:].indirect(L), F.Identity, ["nbw", "nbpad", "tl"], ["nb32"])
            ac(T.lab32[:], T.labf[:].indirect(L), F.Identity, ["labf", "tl"], ["lab32"])
            ac(T.nb32[:, 256:272], T.nb32[:, 0:16], F.Identity, ["nb32"], ["nb32b"])
        least(12, 16)
        diffs(12)
        diffs(13)
        mms([(TH, mat("one"), thr), (TH, mat("n15"), T.ndt[:])], ["one", "n15", "ndt"] + snl, ["#6"])
        least(16, 20)
        diffs(14)
        diffs(15)
        least(20, 24)
        if not last:
            mms([(ZA, mat("one"), T.r2[:, 0:256], True, False), (ZA, mat("one"), T.r1[:, 0:256], False, False),
                 (ZB, mat("one"), T.r2[:, 256:272], True, False), (ZB, mat("one"), T.r1[:, 256:272], False, False)],
                ["one", "r1", "r2"], ["#4", "#5"])
        least(24, 28)
        mms([(DE, mat("l15"), T.ndt[:], True, False), (DE, mat("neg"), old, False, False),
             (KEY, mat("l15"), T.ndt[:], True, False), (KEY, mat("kd"), T.ones[:], False, False)],
            ["l15", "neg", "kd", "ndt", "ones"] + gtl, ["#0", "#1"])
        for a, b in zip((28,) + LAST, LAST + (32,)):
            least(a, b)
        tt(T.up[:], sc, TH, A.is_lt, snn + ["#6"], ["up"])
        mms([(DE, mat("one"), sc, False, True), (KEY, mat("one"), sc, False, False)], ["one"] + snn, ["#0", "#1"])
        if not last:
            mms([(ZA, mat("sum4k"), T.up[:], False, True), (ZB, mat("sum4k"), T.up[:, 0:16], False, True)],
                ["sum4k", "up"], ["#4", "#5"])
        mms([(KEY, mat("n512"), T.up[:], False, True)], ["n512", "up"], ["#1"])
        tt(T.dm[:], T.up[:], DE, A.mult, ["up", "#0"], ["dm"])

        def new_d():
            tt(W[t][:, 0:TW].indirect(L), old, T.dm[:], A.add, gtl + ["dm", "tl"], [wn + "own", wn + "g"])

        def least_key():
            scan(T.ks[:], T.k0[:], T.kt[:], A.max, A.min, ["k0", "kt"], ["ks"], -1000.0)
            ts(T.y2[:, c:256:16], T.ks[:, 15:256:16], ROUND, 257.0 - ROUND, A.add, A.add, ["ks"], ["y2"])

        if last:
            tr32(T.kt[:], KEY, ["#1"], ["kt"])
            new_d()
            dma("y", T.yd[:], W[t][:, 0:V], [wn + "own"], ["yd"])
            least_key()
            tt(T.y1[:, c:256:16], T.ks[:, 15:256:16], T.y2[:, c:256:16], A.subtract, ["ks", "y2"], ["y1"])
            tr32(T.d1[:], T.y1[:], ["y1"], ["d1"])
            ts(T.lo[:].indirect(L), T.d1[:], 32.0, NP - 1.0 + 257.0 * 32.0 - 8.0, A.mult, A.add, ["d1", "tl"], ["lo"])
            dma("s", T.yl[15:128:16, :], T.lo[15:128:16, 0:V], ["lo"], ["yl"])
            break
        tt(T.zz[:], T.nb32[:], ZW, A.max, ["nb32", "nb32b", "#4", "#5"], ["zz"])
        tr32(T.tt[:, 0:256], T.zz[:, 0:256], ["zz"], ["tt0"])
        tr32(T.tt[:, 256:512], T.zz[:, 16:272], ["zz"], ["tt1"])

        def lists(a, b):
            cp(T.xo[:, 16 * a:16 * b], T.tt[:].indirect(T.gl[:, a:b]), ["tt0", "tt1", "gl"], ["xo%d" % i for i in range(a, b)])
        stamp = T.st[:, 256 * t:256 * (t + 1)]
        lists(0, 4)
        for j in range(8):
            i = 4 * (j // 2) + 2 + j % 2
            cp(T.gv[:].indirect(T.xo[:, 16 * i:16 * i + 16]), stamp, ["xo%d" % i, "st%d" % t], ["gv", "gvown"])
            if j < 3:
                lists(4 * j + 4, 4 * j + 8)
            if t == 0:
                slot_columns(j)
        for j in range(8):
            i = 4 * (j // 2) + j % 2
            ac(T.gs[:].indirect(T.xo[:, 16 * i:16 * i + 16]), stamp, F.Silu, ["xo%d" % i, "st%d" % t], ["gs", "gsown"])
            if j == 0 and t == 0:
                scaled(T.idf[:], mat("one"), 1.0, ["one"], ["idf"])
            if j == 1 and t == 0:
                scaled(T.b2[:], T.b3[:], T.eq[:, 0:1], ["b3", "eq"], ["b2"])
            if j == 4:
                ac(W[t + 1][:, 3072:WW], W[0][:, 3072:WW], F.Identity, ["w0rt", "w0none"],
                   ["w%drt" % (t + 1), "w%dnone" % (t + 1)])
        R = T["fr%d" % t]
        for h in range(2):
            a = V + GS * h
            tt(T.ov[:, V * h:V * h + V].indirect(T.lst[:, 32 * h:32 * h + 32]), T.gv[:, a:a + GS], T.gs[:, a:a + GS], A.max,
               ["lst", "gv", "gs", "ov"], ["ov%d" % h])
            ac(T.ow[:, V * h:V * h + V].indirect(T.lst[:, 64:96]), (T.gs, T.gv)[h][:, V + 2 * GS:2 * V], F.Silu,
               ["lst", ("gs", "gv")[h], "ow"], ["ow%d" % h])
            dma("ys"[h], T.xf[:, 192 * h + 96:192 * h + 192], T.ow[0:128:16, V * h:V * h + V], ["ow%d" % h], ["xw%d" % h])
            dma("y", T.xf[:, 192 * h:192 * h + 96], T.ov[0:128:16, V * h:V * h + V], ["ov%d" % h], ["xv%d" % h])
        for h in range(2):
            a = 192 * h
            send([(peer(-1 - h), 0, 2 * q4, T.xf[:, a:a + 96], R[:, a:a + 96]),
                  (peer(-3), 2 * q4, ne, T.xf[:, a + 96:a + 192], R[:, a + 96:a + 192])], "af%d%d" % (t, h),
                 ["xv%d" % h, "xw%d" % h])
        new_d()
        for d in range(1, N):
            pick_d(t, d)
        send_d(t + 1, [1, 2])
        send_d(t + 1, [3])
        dma("y", W[t + 1][:, 0:V], W[t][:, 0:V], [wn + "own"], ["w%down" % (t + 1), "xv1"])
        mms([(FS, T.idf[:], T.rem[:], True, False)]
            + [(FS, lane(T.b2, l), T.gs[:, l:V:16], False, False) for l in range(16)], ["idf", "b2", "rem", "gs"], ["#7"])
        mms([(FS, lane(T.b2, l), T.gv[:, l:V:16], False, False) for l in range(16)], ["b2", "gv"], ["#7"])
        tr32(T.kt[:], KEY, ["#1"], ["kt"])
        least_key()
        tt(T.df[:], T.ks[:, 15:256:16], T.y2[:, c:256:16], A.subtract, ["ks", "y2"], ["df"])
        tr32(T.d2[:], T.y2[:], ["y2"], ["d2"])
        ts(T.y1[:, c:256:16], T.df[:], 32.0, 257.0 * 32.0 - 8.0, A.mult, A.add, ["df"], ["y1"])
        tt(T.ldw[:].indirect(L), T.ldt[:], T.d2[:], A.add, ["ldt", "d2", "tl"], ["ldw", "ldpad"])
        tr32(T.d1[:], T.y1[:], ["y1"], ["d1"])

    num = {}
    for o in ops:
        if o["kind"] == "c" and o["need"]:
            num[o["sem"]] = num.get(o["sem"], 0) + 1
            o["val"] = num[o["sem"]]
    seen, anyq = {}, {}
    for o in ops:
        if o["kind"] == "a":
            continue
        q = o["q"]
        want = {}
        for x in o["deps"]:
            want[x["sem"]] = max(want.get(x["sem"], 0), x["val"])
        for s in want:
            if seen.get((q, s), 0) < want[s]:
                Q[q].wait_ge(T.sem[s], want[s])
                seen[(q, s)] = want[s]
                anyq[s] = max(anyq.get(s, 0), want[s])
        r = o["fn"]()
        if o["kind"] == "c" and o["need"]:
            r.then_inc(T.sem[o["sem"]], 1)
    for o in ops:
        if o["kind"] != "c" and anyq.get(o["sem"], 0) < o["val"]:
            g.wait_ge(T.sem[o["sem"]], o["val"])
